import numpy as np
import ml_dtypes


def mxq(x, axis, fmt="e4m3"):
    dtype, down = {"e4m3": (ml_dtypes.float8_e4m3fn, 7), "e5m2": (ml_dtypes.float8_e5m2, 14)}[fmt]
    v = np.moveaxis(np.asarray(x, np.float32).astype(ml_dtypes.bfloat16).astype(np.float64), axis, -1)
    blocks = v.reshape(v.shape[:-1] + (-1, 32))
    amax = np.abs(blocks).max(-1, keepdims=True)
    byte = np.maximum(np.where(amax > 0, np.frexp(amax)[1] - 1 + 127, 0) - down, 1)
    scale = np.exp2(byte - 127.0)
    codes = (blocks / scale).astype(np.float32).astype(dtype).astype(np.float64)
    return np.moveaxis((codes * scale).reshape(v.shape), -1, axis)


WIDE = False


def mx_kscale(k):
    if not WIDE:
        return np.ones(k)
    levels = np.array([10, -10, 5, -5, 0])
    if k % 512:
        return np.exp2(np.random.permutation(np.resize(levels, k // 32))).repeat(32)
    a = np.empty((k // 512, 16))
    for p in range(k // 512):
        a[p, :8] = np.random.permutation(np.resize(levels, 8))
        for g in range(8):
            far = levels[np.abs(levels - a[p, g]) >= 10]
            a[p, g + 8] = far[np.random.randint(len(far))]
    return np.exp2(a.ravel()).repeat(32)


BF16 = ml_dtypes.bfloat16


def bf(x):
    return np.asarray(x, np.float32).astype(BF16)


def f64(x):
    return np.asarray(x).astype(np.float64)


E2M1 = np.array([0.0, 0.5, 1.0, 1.5, 2.0, 3.0, 4.0, 6.0, -0.0, -0.5, -1.0, -1.5, -2.0, -3.0, -4.0, -6.0])


def pack_weight(w, fmt):
    k, n = w.shape
    w = f64(bf(w)).reshape(k // 32, 32, n)
    amax = np.abs(w).max(1)
    if fmt == "e4m3":
        byte = np.frexp(amax)[1] - 1 + 127 - 7
    else:
        mant, ex = np.frexp(amax / 6.0)
        byte = np.where(mant > 0.5, ex, ex - 1) + 127
    byte = np.clip(np.where(amax > 0, byte, 1), 1, 254)
    scaled = (w * np.exp2(127.0 - byte)[:, None, :]).reshape(k, n).astype(np.float32)
    by_word = np.ascontiguousarray(scaled.reshape(k // 512, 128, 4, n).transpose(0, 1, 3, 2))
    if fmt == "e4m3":
        words = by_word.astype(ml_dtypes.float8_e4m3fn).view(np.uint8)
    else:
        c = by_word.astype(ml_dtypes.float4_e2m1fn).view(np.uint8) & 0xF
        words = c[..., 0::2] | (c[..., 1::2] << 4)
    return np.ascontiguousarray(words), np.ascontiguousarray(byte.astype(np.uint8).reshape(k // 512, 16, n))


def unpack_weight(words, scales, fmt):
    g, p, n, _ = words.shape
    if fmt == "e4m3":
        vals = np.ascontiguousarray(words).view(ml_dtypes.float8_e4m3fn).astype(np.float64)
    else:
        nib = np.empty((g, p, n, 4), np.uint8)
        nib[..., 0::2] = words & 0xF
        nib[..., 1::2] = words >> 4
        vals = E2M1[nib]
    vals = vals * np.repeat(np.exp2(scales.astype(np.float64) - 127.0), 8, axis=1)[..., None]
    return vals.transpose(0, 1, 3, 2).reshape(g * 512, n)
def pack4(w):
    words, scales = pack_weight(w, "e2m1")
    return words.reshape(words.shape[0], 128, -1), scales


def unpack4(words, scales):
    return unpack_weight(words.reshape(words.shape[0], 128, -1, 2), scales, "e2m1")


def planes(Y):
    n, m = Y.shape
    b = f64(bf(Y)).reshape(n // 32, 32, m)
    amax = np.abs(b).max(1)
    byte = np.clip(np.where(amax > 0, np.frexp(amax)[1] - 1 + 127 - 7, 1), 1, 254)
    codes = (b * np.exp2(127.0 - byte)[:, None, :]).reshape(n, m).astype(np.float32).astype(ml_dtypes.float8_e4m3fn).view(np.uint8)
    words = codes.reshape(n // 512, 128, 4, m).transpose(0, 1, 3, 2)
    return np.ascontiguousarray(words), np.ascontiguousarray(byte.astype(np.uint8).reshape(n // 512, 16, m))


T, D, K = 1024, 512, 1024


def neural_features(x, wq, bias):
    return np.tanh((mxq(x, 1, "e4m3") @ wq) + bias[None, :])


def setup_inputs():
    s, t = mx_kscale(D), mx_kscale(T)
    x0 = bf(np.random.standard_normal((T, D)) * s)
    x1 = bf(np.random.standard_normal((T, D)) * s)
    w_words, w_scales = pack4(np.random.standard_normal((D, K)) / np.sqrt(D) / s[:, None])
    return {
        "x0": x0,
        "x1": x1,
        "w_words": w_words,
        "w_scales": w_scales,
        "bias": bf(0.2 * np.random.standard_normal(K)),
        "a": bf(np.exp(0.3 * np.random.standard_normal(T)) * t),
        "b": bf(np.exp(0.3 * np.random.standard_normal(T)) / t),
    }


def core(x0, x1, w_words, w_scales, bias, a, b):
    x0, x1, bias, a, b = f64(x0), f64(x1), f64(bias), f64(a), f64(b)
    wq = unpack4(w_words, w_scales)
    c0 = neural_features(x0, wq, bias)
    c1 = neural_features(x1, wq, bias)
    p = a * b
    z = np.sum(p)
    m0 = np.sum(p[:, None] * c0, axis=0)
    m1 = np.sum(p[:, None] * c1, axis=0)
    left = a[:, None] * c0
    right = b[:, None] * c1
    s = mxq(left, 0, "e4m3").T @ mxq(right, 0, "e4m3")
    return (s - m0[:, None] * m1[None, :] / z) / np.sqrt(z)


def reference(x0, x1, w_words, w_scales, bias, a, b):
    R_out = core(x0, x1, w_words, w_scales, bias, a, b)
    words, scales = planes(R_out)
    return R_out, words, scales

@@ -1,0 +1,565 @@
+from contextlib import ExitStack
+
+import concourse.mybir as mybir
+from concourse.masks import make_identity
+
+T, D, K = 1024, 512, 1024
+P = 128
+BUFS = {"mm": 3, "trv": 2, "trs": 2}
+FLOPS = 2 * (2 * T * D * K) + 2 * K * T * K
+
+F32 = mybir.dt.float32
+BF16 = mybir.dt.bfloat16
+U32 = mybir.dt.uint32
+I32 = mybir.dt.int32
+U8 = mybir.dt.uint8
+FP8X4 = mybir.dt.float8_e4m3fn_x4
+FP4X4 = mybir.dt.float4_e2m1fn_x4
+ADD = mybir.AluOpType.add
+MUL = mybir.AluOpType.mult
+TANH = mybir.ActivationFunctionType.Tanh
+COPY = mybir.ActivationFunctionType.Copy
+AX = mybir.AxisListType.X
+
+
+def tile_girsanovreweightedneurallagcovariance_x2_kernel(
+    tc, x0, x1, w_words, w_scales, bias, a, b, out_0, out_1, out_2
+):
+    nc = tc.nc
+    with ExitStack() as ctx:
+        keep = ctx.enter_context(tc.tile_pool(name="keep", bufs=1))
+        work = ctx.enter_context(tc.tile_pool(name="work", bufs=2))
+        psum = ctx.enter_context(tc.psum_pool(name="psum", bufs=1))
+        ctx.enter_context(tc.manual_schedule())
+
+        w_nat = keep.tile([P, 2 * K], U8, align_bytes=64)
+        ws_nat = keep.tile([P, K], U8, align_bytes=64)
+        nc.gpsimd.memset(ws_nat[:].bitcast(I32), 0)
+        ident = keep.tile([P, P], F32)
+        make_identity(nc, ident[:])
+        ones = keep.tile([P, P], F32)
+        nc.gpsimd.memset(ones[:], 1.0)
+        neg_half = keep.tile([P, 1], F32)
+        nc.gpsimd.memset(neg_half[:], -0.5)
+
+        a_h = keep.tile([P, 8], BF16)
+        b_h = keep.tile([P, 8], BF16)
+        bias_h = keep.tile([P, 8], BF16)
+        for t, v in ((a_h, a), (b_h, b)):
+            nc.scalar.dma_start(out=t[:].rearrange("p (g j) -> p g j", g=2), in_=v.rearrange("(g p j) -> p g j", g=2, j=4))
+        for q in range(4):
+            nc.scalar.dma_start(
+                out=ws_nat[32 * q : 32 * q + 4, :].bitcast(I32), in_=w_scales[0, 4 * q : 4 * q + 4, :].bitcast(I32)
+            )
+        nc.scalar.dma_start(out=bias_h[:].rearrange("p (g j) -> p g j", g=2), in_=bias.rearrange("(g p j) -> p g j", g=2, j=4))
+        af = keep.tile([P, 8], F32)
+        bf = keep.tile([P, 8], F32)
+        pf = keep.tile([P, 8], F32)
+        bias_f = keep.tile([P, 8], F32)
+        nc.sync.dma_start(out=w_nat[:].bitcast(I32), in_=w_words[0].bitcast(I32))
+        xr = {}
+        for name, x in (("x0", x0), ("x1", x1)):
+            for g in range(2):
+                t = keep.tile([P, 4, D], BF16, name="xr_%s_%d" % (name, g), align_bytes=64)
+                xr[name, g] = t
+                src = x[512 * g : 512 * g + 512, :].rearrange("(p j) d -> p j d", j=4)
+                for jp in range(2):
+                    nc.sync.dma_start(out=t[:, 2 * jp : 2 * jp + 2, :], in_=src[:, 2 * jp : 2 * jp + 2, :])
+
+        nc.gpsimd.tensor_tensor(out=pf[:], in0=a_h[:], in1=b_h[:], op=MUL)
+        for t, v in ((bias_f, bias_h), (af, a_h), (bf, b_h)):
+            nc.gpsimd.tensor_copy(out=t[:], in_=v[:])
+
+        w_perm = keep.tile([P, 2 * K], U8, align_bytes=64)
+        ws_perm = keep.tile([P, K], U8, align_bytes=64)
+
+        def permute(g):
+            nc.vector.tensor_copy(
+                out=w_perm[:, 1024 * g : 1024 * g + 1024].rearrange("p (j m b) -> p j m b", j=4, b=2),
+                in_=w_nat[:, 1024 * g : 1024 * g + 1024].rearrange("p (m j b) -> p j m b", j=4, b=2),
+            )
+            nc.vector.tensor_copy(
+                out=ws_perm[:, 512 * g : 512 * g + 512].rearrange("p (j m) -> p j m", j=4),
+                in_=ws_nat[:, 512 * g : 512 * g + 512].rearrange("p (m j) -> p j m", j=4),
+            )
+
+        xq = {}
+        xs = {}
+
+        xbank = {}
+        xt = {}
+
+        def x_tr(name, g, tags):
+            xw = xr[name, g][:].rearrange("p j d -> p (j d)").bitcast(F32)
+            for jp in range(2):
+                bank = psum.tile([P, 512], F32, name=tags[jp], bufs=BUFS[tags[jp]])
+                xbank[name, g, jp] = bank
+                for jj in range(2):
+                    for u in range(2):
+                        j = 2 * jp + jj
+                        nc.tensor.transpose(
+                            bank[:, 256 * jj + 128 * u : 256 * jj + 128 * u + 128],
+                            xw[:, 256 * j + u : 256 * (j + 1) : 2],
+                            ident[:],
+                        )
+
+        def x_evac(name, g, jp, eng):
+            if jp == 0:
+                xt[name, g] = work.tile([P, 2048], BF16, name="xt", bufs=3, align_bytes=64)
+            dst = xt[name, g][:].bitcast(F32)[:, 512 * jp : 512 * jp + 512].rearrange("p (j q u) -> p j q u", j=2, u=2)
+            srcv = xbank[name, g, jp][:].rearrange("p (j u q) -> p j q u", j=2, u=2)
+            if eng == "S":
+                nc.scalar.copy(out=dst, in_=srcv)
+            else:
+                nc.vector.tensor_copy(out=dst, in_=srcv)
+
+        def x_quant(name, g):
+            cq = keep.tile([P, 512], U32, name="xq_%s_%d" % (name, g), align_bytes=64)
+            cs = keep.tile([P, 512], U8, name="xs_%s_%d" % (name, g), align_bytes=64)
+            nc.vector.quantize_mx(out=cq[:].bitcast(FP8X4), scales=cs[:], in_=xt[name, g][:])
+            xq[name, g] = cq
+            xs[name, g] = cs
+
+        ct = {}
+
+        def stage1(name, k, *groups):
+            if 0 in groups:
+                ct[name, k] = work.tile([P, 1024], F32, name="ct_" + name, bufs=8 if name == "x1" else 4)
+            c = ct[name, k]
+            for g in groups:
+                mm = psum.tile([P, 512], F32, name="mm", bufs=BUFS["mm"])
+                nc.tensor.matmul_mx(
+                    out=mm[:],
+                    lhsT=w_perm[:, 256 * k : 256 * k + 256].bitcast(FP4X4),
+                    lhsT_scale=ws_perm[:, 128 * k : 128 * k + 128],
+                    rhs=xq[name, g][:].bitcast(FP8X4),
+                    rhs_scale=xs[name, g][:],
+                    start=True,
+                    stop=True,
+                )
+                nc.scalar.activation(
+                    out=c[:, 512 * g : 512 * g + 512], in_=mm[:], func=TANH, bias=bias_f[:, k : k + 1], scale=1.0
+                )
+
+        m0 = keep.tile([P, 8], F32)
+        lq = [keep.tile([P, 1024], U32, name="lq_%d" % g, align_bytes=64) for g in range(2)]
+        ls = [keep.tile([P, 1024], U8, name="ls_%d" % g, align_bytes=64) for g in range(2)]
+        rq = [keep.tile([P, 1024], U32, name="rq_%d" % g, align_bytes=64) for g in range(2)]
+        rsc = [keep.tile([P, 1024], U8, name="rsc_%d" % g, align_bytes=64) for g in range(2)]
+        small = psum.tile([P, 512], F32, name="small", bufs=1)
+        p_bc = keep.tile([P, 1024], F32)
+        rs = keep.tile([P, 1], F32)
+        nzr = keep.tile([P, 1], F32)
+
+        def weights():
+            for h in range(2):
+                bank = psum.tile([P, 512], F32, name="mm", bufs=BUFS["mm"])
+                for j in range(4):
+                    nc.tensor.matmul(
+                        out=bank[:, 128 * j : 128 * j + 128],
+                        lhsT=pf[:, 4 * h + j : 4 * h + j + 1].to_broadcast([P, P]),
+                        rhs=ident[:],
+                        start=True,
+                        stop=True,
+                    )
+                nc.scalar.copy(out=p_bc[:, 512 * h : 512 * h + 512], in_=bank[:])
+
+        def norm():
+            psum_col = keep.tile([P, 1], F32)
+            nc.vector.reduce_sum(out=psum_col[:], in_=pf[:], axis=AX)
+            nc.tensor.matmul(out=small[:, 0:1], lhsT=ones[:], rhs=psum_col[:], start=True, stop=True)
+            z = keep.tile([P, 1], F32)
+            nc.vector.tensor_copy(out=z[:], in_=small[:, 0:1])
+            nc.gpsimd.tensor_tensor(out=rs[:], in0=z[:], in1=neg_half[:], op=mybir.AluOpType.pow)
+            rs2 = keep.tile([P, 1], F32)
+            nc.gpsimd.tensor_tensor(out=rs2[:], in0=rs[:], in1=rs[:], op=MUL)
+            nc.gpsimd.tensor_scalar(out=nzr[:], in0=rs2[:], scalar1=rs[:, 0:1], scalar2=-1.0, op0=MUL, op1=MUL)
+
+        def c0_m(k):
+            junk = work.tile([P, 1024], BF16, name="junk", bufs=2)
+            nc.vector.scalar_tensor_tensor(
+                out=junk[:], in0=ct["x0", k][:], scalar=1.0, in1=p_bc[:], op0=MUL, op1=MUL, accum_out=m0[:, k : k + 1]
+            )
+
+        lbf = {}
+        banks = {}
+
+        def c0_tr(k, g):
+            bank = psum.tile([P, 512], F32, name="trv", bufs=BUFS["trv"])
+            banks[k, g] = bank
+            for j in range(4):
+                col = 512 * g + 128 * j
+                nc.tensor.transpose(bank[:, 128 * j : 128 * j + 128], ct["x0", k][:, col : col + 128], ident[:])
+
+        def c0_evac(k, g):
+            if k % 2 == 0:
+                lbf[k // 2, g] = work.tile([P, 1024], BF16, name="lbf_%d" % g, bufs=2, align_bytes=64)
+            o = 512 * (k % 2)
+            nc.vector.tensor_tensor(
+                out=lbf[k // 2, g][:, o : o + 512].rearrange("p (q j) -> p q j", j=4),
+                in0=banks[k, g][:].rearrange("p (j q) -> p q j", j=4),
+                in1=af[:, 4 * g : 4 * g + 4].unsqueeze(1).to_broadcast([P, P, 4]),
+                op=MUL,
+            )
+
+        def c0_quant(kp, g):
+            if True:
+                nc.vector.quantize_mx(
+                    out=lq[g][:, 256 * kp : 256 * kp + 256].bitcast(FP8X4),
+                    scales=ls[g][:, 256 * kp : 256 * kp + 256],
+                    in_=lbf[kp, g][:],
+                )
+
+        rf = {}
+
+        def c1_unit(quad, g, j):
+            if j == 0:
+                rf[quad, g] = work.tile([P, 4, 512], F32, name="rf", bufs=3)
+            bank = psum.tile([P, 512], F32, name="trs", bufs=BUFS["trs"])
+            col = 512 * g + 128 * j
+            for jf in range(4):
+                nc.tensor.transpose(
+                    bank[:, 128 * jf : 128 * jf + 128], ct["x1", 4 * quad + jf][:, col : col + 128], ident[:]
+                )
+            nc.scalar.activation(
+                out=rf[quad, g][:, j, :].rearrange("p (q f) -> p q f", f=4),
+                in_=bank[:].rearrange("p (f q) -> p q f", f=4),
+                func=COPY,
+                scale=bf[:, 4 * g + j : 4 * g + j + 1],
+            )
+
+        rbf = {}
+
+        def c1_inter(quad, g):
+            t = work.tile([P, 2048], BF16, name="rbf", bufs=2, align_bytes=64)
+            rbf[quad, g] = t
+            nc.vector.tensor_copy(
+                out=t[:].rearrange("p (n j) -> p n j", j=4), in_=rf[quad, g][:].rearrange("p j n -> p n j")
+            )
+
+        def c1_sum(quad, g, blks):
+            for blk in blks:
+                c = 8 + 2 * (4 * quad + blk) + g
+                for j in range(4):
+                    nc.tensor.matmul(
+                        out=small[:, c : c + 1],
+                        lhsT=rf[quad, g][:, j, 128 * blk : 128 * blk + 128],
+                        rhs=af[:, 4 * g + j : 4 * g + j + 1],
+                        start=(j == 0),
+                        stop=(j == 3),
+                    )
+
+        def c1_quant(quad, g):
+            nc.vector.quantize_mx(
+                out=rq[g][:, 512 * quad : 512 * quad + 512].bitcast(FP8X4),
+                scales=rsc[g][:, 512 * quad : 512 * quad + 512],
+                in_=rbf[quad, g][:],
+            )
+
+        m1_bc = keep.tile([P, 1024], F32)
+
+        m1s = {}
+
+        def m1_red(quad):
+            m1 = keep.tile([P, 4], F32, name="m1_%d" % quad)
+            m1s[quad] = m1
+            nc.vector.reduce_sum(
+                out=m1[:], in_=small[:, 8 + 8 * quad : 16 + 8 * quad].rearrange("p (k g) -> p k g", g=2), axis=AX
+            )
+
+        def m1_spread(quad):
+            m1 = m1s[quad]
+            bank = psum.tile([P, 512], F32, name="trs", bufs=BUFS["trs"])
+            for blk in range(4):
+                nc.tensor.matmul(
+                    out=bank[:, 128 * blk : 128 * blk + 128],
+                    lhsT=m1[:, blk : blk + 1].to_broadcast([P, P]),
+                    rhs=ident[:],
+                    start=True,
+                    stop=True,
+                )
+            nc.scalar.copy(out=m1_bc[:, 512 * quad : 512 * quad + 512], in_=bank[:])
+
+        res = {}
+        gm = {}
+
+        def rank1(k, h):
+            t = work.tile([P, 512], F32, name="gm", bufs=8)
+            gm[k, h] = t
+            nc.gpsimd.tensor_scalar(
+                out=t[:], in0=m1_bc[:, 512 * h : 512 * h + 512], scalar1=m0[:, k : k + 1], scalar2=nzr[:, 0:1], op0=MUL, op1=MUL
+            )
+
+        s_bank = {}
+
+        def stage2_mx(k, h):
+            mm = psum.tile([P, 512], F32, name="mm", bufs=BUFS["mm"])
+            s_bank[k, h] = mm
+            for g in range(2):
+                nc.tensor.matmul_mx(
+                    out=mm[:],
+                    lhsT=lq[g][:, 128 * k : 128 * k + 128].bitcast(FP8X4),
+                    lhsT_scale=ls[g][:, 128 * k : 128 * k + 128],
+                    rhs=rq[g][:, 512 * h : 512 * h + 512].bitcast(FP8X4),
+                    rhs_scale=rsc[g][:, 512 * h : 512 * h + 512],
+                    start=(g == 0),
+                    stop=(g == 1),
+                )
+
+        def stage2_out(k, h):
+            quad, j = divmod(k, 4)
+            if j == 0:
+                res[quad, h] = work.tile([P, 4, 512], F32, name="res", bufs=4)
+            nc.vector.scalar_tensor_tensor(
+                out=res[quad, h][:, j, :], in0=s_bank[k, h][:], scalar=rs[:, 0:1], in1=gm[k, h][:], op0=MUL, op1=ADD
+            )
+            nc.sync.dma_start(
+                out=out_0[512 * quad : 512 * quad + 512, :].rearrange("(p j) n -> p j n", j=4)[:, j, 512 * h : 512 * h + 512],
+                in_=res[quad, h][:, j, :],
+            )
+
+        ybf = {}
+        yq = {}
+
+        def planes_inter(quad, h, c0, c1, eng):
+            if (quad, h) not in ybf:
+                ybf[quad, h] = work.tile([P, 2048], BF16, name="ybf", bufs=2, align_bytes=64)
+            dst = ybf[quad, h][:, 4 * c0 : 4 * c1].rearrange("p (n j) -> p n j", j=4)
+            srcv = res[quad, h][:, :, c0:c1].rearrange("p j n -> p n j")
+            if eng == "S":
+                nc.scalar.copy(out=dst, in_=srcv)
+            else:
+                nc.vector.tensor_copy(out=dst, in_=srcv)
+
+        def planes_quant(quad, h, c0, c1):
+            if (quad, h) not in yq:
+                yq[quad, h] = (
+                    work.tile([P, 512], U32, name="yq", bufs=2, align_bytes=64),
+                    work.tile([P, 512], U8, name="ys", bufs=2, align_bytes=64),
+                )
+            codes, scales = yq[quad, h]
+            nc.vector.quantize_mx(
+                out=codes[:, c0:c1].bitcast(FP8X4), scales=scales[:, c0:c1], in_=ybf[quad, h][:, 4 * c0 : 4 * c1]
+            )
+            nc.sync.dma_start(
+                out=out_1[quad].rearrange("p m t -> p (m t)").bitcast(I32)[:, 512 * h + c0 : 512 * h + c1],
+                in_=codes[:, c0:c1].bitcast(I32),
+            )
+
+        def planes_scales(quad, h):
+            scales = yq[quad, h][1]
+            for q in range(4):
+                nc.sync.dma_start(
+                    out=out_2[quad, 4 * q : 4 * q + 4, 512 * h : 512 * h + 512].bitcast(I32),
+                    in_=scales[32 * q : 32 * q + 4, :].bitcast(I32),
+                )
+
+        weights()
+        x_tr("x0", 0, ("trs", "trv"))
+        permute(0)
+        x_tr("x0", 1, ("trs", "trv"))
+        x_evac("x0", 0, 0, "S")
+        x_evac("x0", 0, 1, "V")
+        x_tr("x1", 0, ("trs", "trv"))
+        x_evac("x0", 1, 0, "S")
+        x_quant("x0", 0)
+        x_evac("x0", 1, 1, "V")
+        x_evac("x1", 0, 0, "S")
+        stage1("x0", 0, 0)
+        x_tr("x1", 1, ("trs", "trv"))
+        x_evac("x1", 1, 0, "S")
+        x_quant("x0", 1)
+        stage1("x0", 0, 1)
+        x_evac("x1", 0, 1, "V")
+        x_evac("x1", 1, 1, "V")
+        stage1("x0", 1, 0)
+        c0_tr(0, 0)
+        x_quant("x1", 0)
+        x_quant("x1", 1)
+        stage1("x0", 1, 1)
+        c0_evac(0, 0)
+        stage1("x0", 2, 0)
+        c0_tr(0, 1)
+        permute(1)
+        c0_evac(0, 1)
+        stage1("x1", 0, 0)
+        stage1("x1", 0, 1)
+        c0_tr(1, 0)
+        stage1("x1", 1, 0)
+        stage1("x0", 2, 1)
+        c0_evac(1, 0)
+        c0_m(0)
+        c0_quant(0, 0)
+        stage1("x1", 1, 1)
+        c0_tr(1, 1)
+        stage1("x1", 2, 0)
+        c0_tr(2, 0)
+        stage1("x1", 2, 1)
+        c0_evac(1, 1)
+        stage1("x1", 3, 0)
+        stage1("x0", 3, 0)
+        stage1("x0", 3, 1)
+        c1_unit(0, 0, 0)
+        c0_tr(2, 1)
+        c0_evac(2, 0)
+        c1_unit(0, 0, 1)
+        norm()
+        c0_evac(2, 1)
+        c0_tr(3, 0)
+        c0_evac(3, 0)
+        stage1("x0", 4, 0)
+        stage1("x1", 3, 1)
+        stage1("x1", 4, 0)
+        c1_unit(0, 0, 2)
+        c0_m(1)
+        c0_tr(3, 1)
+        c0_quant(0, 1)
+        c1_unit(0, 0, 3)
+        stage1("x1", 4, 1)
+        stage1("x1", 5, 0)
+        stage1("x0", 4, 1)
+        c0_tr(4, 0)
+        c0_evac(3, 1)
+        c1_unit(0, 1, 0)
+        c1_sum(0, 0, (0,))
+        c1_sum(0, 0, (1,))
+        c1_unit(0, 1, 1)
+        c1_sum(0, 0, (2,))
+        c0_evac(4, 0)
+        stage1("x0", 5, 0)
+        c1_inter(0, 0)
+        stage1("x1", 5, 1)
+        c0_quant(1, 0)
+        c0_m(2)
+        c1_quant(0, 0)
+        stage1("x1", 6, 0)
+        c1_unit(0, 1, 2)
+        c0_tr(4, 1)
+        c1_sum(0, 0, (3,))
+        c0_m(3)
+        c0_tr(5, 0)
+        c1_unit(0, 1, 3)
+        stage1("x1", 6, 1)
+        stage1("x1", 7, 0)
+        stage1("x0", 5, 1)
+        c1_sum(0, 1, (0,))
+        c1_sum(0, 1, (1,))
+        c0_evac(4, 1)
+        c1_sum(0, 1, (2,))
+        c1_unit(1, 0, 0)
+        stage1("x0", 6, 0)
+        c0_m(4)
+        c1_inter(0, 1)
+        stage1("x0", 6, 1)
+        c0_evac(5, 0)
+        c1_sum(0, 1, (3,))
+        c1_quant(0, 1)
+        c1_unit(1, 0, 1)
+        c0_quant(1, 1)
+        c0_tr(5, 1)
+        c1_unit(1, 0, 2)
+        c0_m(5)
+        c0_tr(6, 0)
+        stage1("x0", 7, 0)
+        m1_red(0)
+        c0_quant(2, 0)
+        c0_evac(5, 1)
+        c0_m(6)
+        stage1("x0", 7, 1)
+        stage1("x1", 7, 1)
+        c1_unit(1, 0, 3)
+        m1_spread(0)
+        c0_evac(6, 0)
+        stage2_mx(0, 0)
+        stage2_mx(1, 0)
+        c0_m(7)
+        stage2_mx(2, 0)
+        c1_unit(1, 1, 0)
+        rank1(0, 0)
+        rank1(1, 0)
+        rank1(2, 0)
+        c1_inter(1, 0)
+        rank1(3, 0)
+        c0_tr(6, 1)
+        stage2_out(0, 0)
+        rank1(4, 0)
+        c0_tr(7, 0)
+        c1_sum(1, 0, (0,))
+        c0_evac(6, 1)
+        c1_sum(1, 0, (1,))
+        c1_unit(1, 1, 1)
+        c1_unit(1, 1, 2)
+        rank1(5, 0)
+        c1_sum(1, 0, (2,))
+        c0_tr(7, 1)
+        c1_unit(1, 1, 3)
+        stage2_out(1, 0)
+        c0_evac(7, 0)
+        c1_sum(1, 0, (3,))
+        stage2_mx(3, 0)
+        c0_quant(2, 1)
+        c1_quant(1, 0)
+        rank1(6, 0)
+        c1_sum(1, 1, (0,))
+        stage2_out(2, 0)
+        c1_sum(1, 1, (1,))
+        rank1(7, 0)
+        c0_evac(7, 1)
+        stage2_out(3, 0)
+        c1_sum(1, 1, (2,))
+        planes_inter(0, 0, 0, 256, "S")
+        c0_quant(3, 0)
+        c1_sum(1, 1, (3,))
+        c1_inter(1, 1)
+        stage2_mx(4, 0)
+        planes_inter(0, 0, 256, 512, "S")
+        stage2_mx(5, 0)
+        m1_red(1)
+        c0_quant(3, 1)
+        m1_spread(1)
+        rank1(0, 1)
+        rank1(1, 1)
+        stage2_out(4, 0)
+        c1_quant(1, 1)
+        stage2_out(5, 0)
+        stage2_mx(6, 0)
+        stage2_out(6, 0)
+        stage2_mx(7, 0)
+        rank1(2, 1)
+        stage2_out(7, 0)
+        stage2_mx(0, 1)
+        planes_quant(0, 0, 0, 512)
+        stage2_mx(1, 1)
+        planes_inter(1, 0, 0, 256, "S")
+        stage2_out(0, 1)
+        stage2_out(1, 1)
+        planes_inter(1, 0, 256, 512, "S")
+        rank1(3, 1)
+        stage2_mx(2, 1)
+        rank1(4, 1)
+        stage2_mx(3, 1)
+        stage2_out(2, 1)
+        rank1(5, 1)
+        stage2_mx(4, 1)
+        rank1(6, 1)
+        stage2_out(3, 1)
+        planes_inter(0, 1, 0, 256, "S")
+        stage2_mx(5, 1)
+        planes_scales(0, 0)
+        stage2_out(4, 1)
+        planes_inter(0, 1, 256, 512, "S")
+        rank1(7, 1)
+        planes_quant(1, 0, 0, 512)
+        stage2_mx(6, 1)
+        stage2_mx(7, 1)
+        planes_scales(1, 0)
+        stage2_out(5, 1)
+        stage2_out(6, 1)
+        stage2_out(7, 1)
+        planes_inter(1, 1, 0, 256, "V")
+        planes_quant(0, 1, 0, 512)
+        planes_scales(0, 1)
+        planes_quant(1, 1, 0, 256)
+        planes_inter(1, 1, 256, 512, "S")
+        planes_quant(1, 1, 256, 512)
+        planes_scales(1, 1)

@@ -5,7 +5,7 @@ from concourse.masks import make_identity
 
 T, D, K = 1024, 512, 1024
 P = 128
-BUFS = {"mm": 3, "trv": 2, "trs": 2}
+BUFS = {"ps": 7, "acc": 1}
 FLOPS = 2 * (2 * T * D * K) + 2 * K * T * K
 
 F32 = mybir.dt.float32
@@ -89,10 +89,10 @@ def tile_girsanovreweightedneurallagcovariance_x2_kernel(
         xbank = {}
         xt = {}
 
-        def x_tr(name, g, tags):
+        def x_tr(name, g, jps):
             xw = xr[name, g][:].rearrange("p j d -> p (j d)").bitcast(F32)
-            for jp in range(2):
-                bank = psum.tile([P, 512], F32, name=tags[jp], bufs=BUFS[tags[jp]])
+            for jp in jps:
+                bank = psum.tile([P, 512], F32, name="ps", bufs=BUFS["ps"])
                 xbank[name, g, jp] = bank
                 for jj in range(2):
                     for u in range(2):
@@ -127,7 +127,7 @@ def tile_girsanovreweightedneurallagcovariance_x2_kernel(
                 ct[name, k] = work.tile([P, 1024], F32, name="ct_" + name, bufs=8 if name == "x1" else 4)
             c = ct[name, k]
             for g in groups:
-                mm = psum.tile([P, 512], F32, name="mm", bufs=BUFS["mm"])
+                mm = psum.tile([P, 512], F32, name="ps", bufs=BUFS["ps"])
                 nc.tensor.matmul_mx(
                     out=mm[:],
                     lhsT=w_perm[:, 256 * k : 256 * k + 256].bitcast(FP4X4),
@@ -146,14 +146,13 @@ def tile_girsanovreweightedneurallagcovariance_x2_kernel(
         ls = [keep.tile([P, 1024], U8, name="ls_%d" % g, align_bytes=64) for g in range(2)]
         rq = [keep.tile([P, 1024], U32, name="rq_%d" % g, align_bytes=64) for g in range(2)]
         rsc = [keep.tile([P, 1024], U8, name="rsc_%d" % g, align_bytes=64) for g in range(2)]
-        small = psum.tile([P, 512], F32, name="small", bufs=1)
         p_bc = keep.tile([P, 1024], F32)
         rs = keep.tile([P, 1], F32)
         nzr = keep.tile([P, 1], F32)
 
         def weights():
             for h in range(2):
-                bank = psum.tile([P, 512], F32, name="mm", bufs=BUFS["mm"])
+                bank = psum.tile([P, 512], F32, name="ps", bufs=BUFS["ps"])
                 for j in range(4):
                     nc.tensor.matmul(
                         out=bank[:, 128 * j : 128 * j + 128],
@@ -167,6 +166,7 @@ def tile_girsanovreweightedneurallagcovariance_x2_kernel(
         def norm():
             psum_col = keep.tile([P, 1], F32)
             nc.vector.reduce_sum(out=psum_col[:], in_=pf[:], axis=AX)
+            small = psum.tile([P, 512], F32, name="ps", bufs=BUFS["ps"])
             nc.tensor.matmul(out=small[:, 0:1], lhsT=ones[:], rhs=psum_col[:], start=True, stop=True)
             z = keep.tile([P, 1], F32)
             nc.vector.tensor_copy(out=z[:], in_=small[:, 0:1])
@@ -185,7 +185,7 @@ def tile_girsanovreweightedneurallagcovariance_x2_kernel(
         banks = {}
 
         def c0_tr(k, g):
-            bank = psum.tile([P, 512], F32, name="trv", bufs=BUFS["trv"])
+            bank = psum.tile([P, 512], F32, name="ps", bufs=BUFS["ps"])
             banks[k, g] = bank
             for j in range(4):
                 col = 512 * g + 128 * j
@@ -215,7 +215,7 @@ def tile_girsanovreweightedneurallagcovariance_x2_kernel(
         def c1_unit(quad, g, j):
             if j == 0:
                 rf[quad, g] = work.tile([P, 4, 512], F32, name="rf", bufs=3)
-            bank = psum.tile([P, 512], F32, name="trs", bufs=BUFS["trs"])
+            bank = psum.tile([P, 512], F32, name="ps", bufs=BUFS["ps"])
             col = 512 * g + 128 * j
             for jf in range(4):
                 nc.tensor.transpose(
@@ -234,20 +234,34 @@ def tile_girsanovreweightedneurallagcovariance_x2_kernel(
             t = work.tile([P, 2048], BF16, name="rbf", bufs=2, align_bytes=64)
             rbf[quad, g] = t
             nc.vector.tensor_copy(
-                out=t[:].rearrange("p (n j) -> p n j", j=4), in_=rf[quad, g][:].rearrange("p j n -> p n j")
+                out=t[:].rearrange("p (c i j) -> p c j i", i=4, j=4),
+                in_=rf[quad, g][:].rearrange("p j (c i) -> p c j i", i=4),
             )
 
-        def c1_sum(quad, g, blks):
-            for blk in blks:
-                c = 8 + 2 * (4 * quad + blk) + g
-                for j in range(4):
-                    nc.tensor.matmul(
-                        out=small[:, c : c + 1],
-                        lhsT=rf[quad, g][:, j, 128 * blk : 128 * blk + 128],
-                        rhs=af[:, 4 * g + j : 4 * g + j + 1],
-                        start=(j == 0),
-                        stop=(j == 3),
-                    )
+        acc = {}
+        m1_bc = keep.tile([P, 1024], F32)
+
+        def c1_sum(quad, g, j):
+            if (g, j) == (0, 0):
+                acc[quad] = psum.tile([P, 512], F32, name="acc", bufs=BUFS["acc"])
+            nc.tensor.matmul(
+                out=acc[quad][:],
+                lhsT=af[:, 4 * g + j : 4 * g + j + 1].to_broadcast([P, P]),
+                rhs=rf[quad, g][:, j, :],
+                start=((g, j) == (0, 0)),
+                stop=((g, j) == (1, 3)),
+            )
+
+        def m1_take(quad):
+            nc.scalar.copy(out=m1_bc[:, 512 * quad : 512 * quad + 512], in_=acc[quad][:])
+
+        m1 = keep.tile([P, 8], F32)
+
+        def c1_m(k):
+            junk = work.tile([P, 1024], BF16, name="junk", bufs=2)
+            nc.vector.scalar_tensor_tensor(
+                out=junk[:], in0=ct["x1", k][:], scalar=1.0, in1=p_bc[:], op0=MUL, op1=MUL, accum_out=m1[:, k : k + 1]
+            )
 
         def c1_quant(quad, g):
             nc.vector.quantize_mx(
@@ -256,29 +270,20 @@ def tile_girsanovreweightedneurallagcovariance_x2_kernel(
                 in_=rbf[quad, g][:],
             )
 
-        m1_bc = keep.tile([P, 1024], F32)
-
-        m1s = {}
-
-        def m1_red(quad):
-            m1 = keep.tile([P, 4], F32, name="m1_%d" % quad)
-            m1s[quad] = m1
-            nc.vector.reduce_sum(
-                out=m1[:], in_=small[:, 8 + 8 * quad : 16 + 8 * quad].rearrange("p (k g) -> p k g", g=2), axis=AX
-            )
-
         def m1_spread(quad):
-            m1 = m1s[quad]
-            bank = psum.tile([P, 512], F32, name="trs", bufs=BUFS["trs"])
-            for blk in range(4):
+            bank = psum.tile([P, 512], F32, name="ps", bufs=BUFS["ps"])
+            for f in range(4):
                 nc.tensor.matmul(
-                    out=bank[:, 128 * blk : 128 * blk + 128],
-                    lhsT=m1[:, blk : blk + 1].to_broadcast([P, P]),
+                    out=bank[:, 128 * f : 128 * f + 128],
+                    lhsT=m1[:, 4 * quad + f : 4 * quad + f + 1].to_broadcast([P, P]),
                     rhs=ident[:],
                     start=True,
                     stop=True,
                 )
-            nc.scalar.copy(out=m1_bc[:, 512 * quad : 512 * quad + 512], in_=bank[:])
+            nc.scalar.copy(
+                out=m1_bc[:, 512 * quad : 512 * quad + 512].rearrange("p (q f) -> p q f", f=4),
+                in_=bank[:].rearrange("p (f q) -> p q f", f=4),
+            )
 
         res = {}
         gm = {}
@@ -293,7 +298,7 @@ def tile_girsanovreweightedneurallagcovariance_x2_kernel(
         s_bank = {}
 
         def stage2_mx(k, h):
-            mm = psum.tile([P, 512], F32, name="mm", bufs=BUFS["mm"])
+            mm = psum.tile([P, 512], F32, name="ps", bufs=BUFS["ps"])
             s_bank[k, h] = mm
             for g in range(2):
                 nc.tensor.matmul_mx(
@@ -324,8 +329,8 @@ def tile_girsanovreweightedneurallagcovariance_x2_kernel(
         def planes_inter(quad, h, c0, c1, eng):
             if (quad, h) not in ybf:
                 ybf[quad, h] = work.tile([P, 2048], BF16, name="ybf", bufs=2, align_bytes=64)
-            dst = ybf[quad, h][:, 4 * c0 : 4 * c1].rearrange("p (n j) -> p n j", j=4)
-            srcv = res[quad, h][:, :, c0:c1].rearrange("p j n -> p n j")
+            dst = ybf[quad, h][:, 4 * c0 : 4 * c1].rearrange("p (c i j) -> p c j i", i=4, j=4)
+            srcv = res[quad, h][:, :, c0:c1].rearrange("p j (c i) -> p c j i", i=4)
             if eng == "S":
                 nc.scalar.copy(out=dst, in_=srcv)
             else:
@@ -354,212 +359,210 @@ def tile_girsanovreweightedneurallagcovariance_x2_kernel(
                     in_=scales[32 * q : 32 * q + 4, :].bitcast(I32),
                 )
 
-        weights()
-        x_tr("x0", 0, ("trs", "trv"))
         permute(0)
-        x_tr("x0", 1, ("trs", "trv"))
+        weights()
+        x_tr("x0", 0, (0,))
+        permute(1)
         x_evac("x0", 0, 0, "S")
-        x_evac("x0", 0, 1, "V")
-        x_tr("x1", 0, ("trs", "trv"))
-        x_evac("x0", 1, 0, "S")
+        x_tr("x0", 0, (1,))
+        x_tr("x0", 1, (0,))
+        x_evac("x0", 0, 1, "S")
+        norm()
+        x_tr("x0", 1, (1,))
+        x_evac("x0", 1, 0, "V")
+        x_evac("x0", 1, 1, "S")
+        x_tr("x1", 0, (0,))
+        x_tr("x1", 0, (1,))
+        x_tr("x1", 1, (0,))
         x_quant("x0", 0)
-        x_evac("x0", 1, 1, "V")
-        x_evac("x1", 0, 0, "S")
-        stage1("x0", 0, 0)
-        x_tr("x1", 1, ("trs", "trv"))
-        x_evac("x1", 1, 0, "S")
         x_quant("x0", 1)
+        x_evac("x1", 0, 0, "S")
+        x_evac("x1", 0, 1, "S")
+        x_evac("x1", 1, 0, "S")
+        stage1("x0", 0, 0)
+        x_tr("x1", 1, (1,))
         stage1("x0", 0, 1)
-        x_evac("x1", 0, 1, "V")
-        x_evac("x1", 1, 1, "V")
         stage1("x0", 1, 0)
+        stage1("x0", 1, 1)
         c0_tr(0, 0)
         x_quant("x1", 0)
-        x_quant("x1", 1)
-        stage1("x0", 1, 1)
-        c0_evac(0, 0)
+        x_evac("x1", 1, 1, "V")
         stage1("x0", 2, 0)
-        c0_tr(0, 1)
-        permute(1)
-        c0_evac(0, 1)
-        stage1("x1", 0, 0)
-        stage1("x1", 0, 1)
-        c0_tr(1, 0)
-        stage1("x1", 1, 0)
         stage1("x0", 2, 1)
-        c0_evac(1, 0)
+        x_quant("x1", 1)
+        stage1("x1", 0, 0)
         c0_m(0)
-        c0_quant(0, 0)
+        c0_tr(0, 1)
+        c0_evac(0, 0)
+        c0_tr(1, 0)
+        stage1("x1", 0, 1)
+        c0_evac(0, 1)
+        stage1("x1", 1, 0)
         stage1("x1", 1, 1)
+        c0_evac(1, 0)
         c0_tr(1, 1)
-        stage1("x1", 2, 0)
         c0_tr(2, 0)
-        stage1("x1", 2, 1)
-        c0_evac(1, 1)
-        stage1("x1", 3, 0)
+        stage1("x1", 2, 0)
+        c0_m(1)
         stage1("x0", 3, 0)
         stage1("x0", 3, 1)
-        c1_unit(0, 0, 0)
+        c0_evac(1, 1)
+        stage1("x1", 2, 1)
         c0_tr(2, 1)
         c0_evac(2, 0)
-        c1_unit(0, 0, 1)
-        norm()
-        c0_evac(2, 1)
-        c0_tr(3, 0)
-        c0_evac(3, 0)
-        stage1("x0", 4, 0)
-        stage1("x1", 3, 1)
-        stage1("x1", 4, 0)
-        c1_unit(0, 0, 2)
-        c0_m(1)
-        c0_tr(3, 1)
-        c0_quant(0, 1)
-        c1_unit(0, 0, 3)
-        stage1("x1", 4, 1)
-        stage1("x1", 5, 0)
-        stage1("x0", 4, 1)
-        c0_tr(4, 0)
-        c0_evac(3, 1)
-        c1_unit(0, 1, 0)
-        c1_sum(0, 0, (0,))
-        c1_sum(0, 0, (1,))
-        c1_unit(0, 1, 1)
-        c1_sum(0, 0, (2,))
-        c0_evac(4, 0)
-        stage1("x0", 5, 0)
-        c1_inter(0, 0)
-        stage1("x1", 5, 1)
-        c0_quant(1, 0)
         c0_m(2)
-        c1_quant(0, 0)
-        stage1("x1", 6, 0)
-        c1_unit(0, 1, 2)
-        c0_tr(4, 1)
-        c1_sum(0, 0, (3,))
+        stage1("x1", 3, 0)
+        c0_quant(0, 0)
+        stage1("x0", 4, 0)
+        c0_tr(3, 0)
+        stage1("x1", 3, 1)
+        c0_evac(2, 1)
+        stage1("x0", 4, 1)
+        c0_tr(3, 1)
+        c1_unit(0, 0, 0)
+        stage1("x1", 4, 0)
+        c0_evac(3, 0)
+        stage1("x1", 4, 1)
+        c0_quant(0, 1)
+        c0_tr(4, 0)
+        c1_unit(0, 0, 1)
+        c0_evac(3, 1)
+        c1_unit(0, 0, 2)
+        c1_sum(0, 0, 0)
         c0_m(3)
+        c0_evac(4, 0)
+        c1_unit(0, 0, 3)
+        c0_m(4)
+        c1_m(4)
+        stage1("x0", 5, 0)
+        c0_tr(4, 1)
+        stage1("x1", 5, 0)
+        c0_quant(1, 0)
+        stage1("x0", 5, 1)
+        stage1("x0", 6, 0)
+        stage1("x1", 5, 1)
+        c0_evac(4, 1)
+        c1_inter(0, 0)
+        c0_m(5)
+        stage1("x1", 6, 0)
         c0_tr(5, 0)
+        c1_unit(0, 1, 0)
+        c0_tr(5, 1)
+        c1_unit(0, 1, 1)
+        c1_unit(0, 1, 2)
+        c1_sum(0, 0, 1)
+        c0_evac(5, 0)
         c1_unit(0, 1, 3)
         stage1("x1", 6, 1)
-        stage1("x1", 7, 0)
-        stage1("x0", 5, 1)
-        c1_sum(0, 1, (0,))
-        c1_sum(0, 1, (1,))
-        c0_evac(4, 1)
-        c1_sum(0, 1, (2,))
-        c1_unit(1, 0, 0)
-        stage1("x0", 6, 0)
-        c0_m(4)
-        c1_inter(0, 1)
         stage1("x0", 6, 1)
-        c0_evac(5, 0)
-        c1_sum(0, 1, (3,))
-        c1_quant(0, 1)
-        c1_unit(1, 0, 1)
         c0_quant(1, 1)
-        c0_tr(5, 1)
-        c1_unit(1, 0, 2)
-        c0_m(5)
-        c0_tr(6, 0)
         stage1("x0", 7, 0)
-        m1_red(0)
-        c0_quant(2, 0)
         c0_evac(5, 1)
-        c0_m(6)
+        c1_m(5)
         stage1("x0", 7, 1)
+        stage1("x1", 7, 0)
         stage1("x1", 7, 1)
-        c1_unit(1, 0, 3)
-        m1_spread(0)
+        c0_quant(2, 0)
+        c1_quant(0, 0)
+        c0_tr(6, 0)
+        c1_sum(0, 0, 2)
+        c1_sum(0, 0, 3)
+        c1_m(6)
+        c0_m(6)
+        c1_sum(0, 1, 0)
         c0_evac(6, 0)
-        stage2_mx(0, 0)
-        stage2_mx(1, 0)
+        c0_tr(6, 1)
+        c1_unit(1, 0, 0)
+        c1_unit(1, 0, 1)
+        c1_unit(1, 0, 2)
+        c1_sum(0, 1, 1)
+        c0_quant(2, 1)
         c0_m(7)
-        stage2_mx(2, 0)
+        c1_inter(0, 1)
+        c1_unit(1, 0, 3)
+        c0_tr(7, 0)
         c1_unit(1, 1, 0)
+        c1_sum(0, 1, 2)
+        c1_sum(0, 1, 3)
+        m1_take(0)
         rank1(0, 0)
+        c1_m(7)
+        c0_evac(6, 1)
         rank1(1, 0)
         rank1(2, 0)
-        c1_inter(1, 0)
-        rank1(3, 0)
-        c0_tr(6, 1)
-        stage2_out(0, 0)
-        rank1(4, 0)
-        c0_tr(7, 0)
-        c1_sum(1, 0, (0,))
-        c0_evac(6, 1)
-        c1_sum(1, 0, (1,))
-        c1_unit(1, 1, 1)
-        c1_unit(1, 1, 2)
-        rank1(5, 0)
-        c1_sum(1, 0, (2,))
         c0_tr(7, 1)
-        c1_unit(1, 1, 3)
-        stage2_out(1, 0)
+        c1_unit(1, 1, 1)
         c0_evac(7, 0)
-        c1_sum(1, 0, (3,))
-        stage2_mx(3, 0)
-        c0_quant(2, 1)
-        c1_quant(1, 0)
-        rank1(6, 0)
-        c1_sum(1, 1, (0,))
-        stage2_out(2, 0)
-        c1_sum(1, 1, (1,))
-        rank1(7, 0)
-        c0_evac(7, 1)
-        stage2_out(3, 0)
-        c1_sum(1, 1, (2,))
-        planes_inter(0, 0, 0, 256, "S")
+        c1_unit(1, 1, 2)
+        c1_inter(1, 0)
+        c1_quant(0, 1)
+        rank1(3, 0)
         c0_quant(3, 0)
-        c1_sum(1, 1, (3,))
-        c1_inter(1, 1)
-        stage2_mx(4, 0)
-        planes_inter(0, 0, 256, 512, "S")
-        stage2_mx(5, 0)
-        m1_red(1)
-        c0_quant(3, 1)
+        c1_unit(1, 1, 3)
+        c0_evac(7, 1)
+        stage2_mx(0, 0)
+        c1_quant(1, 0)
+        stage2_mx(1, 0)
+        stage2_mx(2, 0)
         m1_spread(1)
+        rank1(4, 0)
+        stage2_mx(3, 0)
+        c0_quant(3, 1)
+        stage2_out(0, 0)
+        stage2_mx(4, 0)
+        stage2_mx(5, 0)
+        stage2_out(1, 0)
+        c1_inter(1, 1)
+        stage2_out(2, 0)
+        stage2_mx(6, 0)
+        stage2_out(3, 0)
+        stage2_mx(7, 0)
+        stage2_out(4, 0)
+        rank1(5, 0)
+        c1_quant(1, 1)
+        rank1(6, 0)
+        rank1(7, 0)
+        stage2_out(5, 0)
         rank1(0, 1)
         rank1(1, 1)
-        stage2_out(4, 0)
-        c1_quant(1, 1)
-        stage2_out(5, 0)
-        stage2_mx(6, 0)
-        stage2_out(6, 0)
-        stage2_mx(7, 0)
-        rank1(2, 1)
-        stage2_out(7, 0)
         stage2_mx(0, 1)
-        planes_quant(0, 0, 0, 512)
+        stage2_out(6, 0)
+        planes_inter(0, 0, 0, 256, "S")
         stage2_mx(1, 1)
-        planes_inter(1, 0, 0, 256, "S")
-        stage2_out(0, 1)
-        stage2_out(1, 1)
-        planes_inter(1, 0, 256, 512, "S")
+        rank1(2, 1)
         rank1(3, 1)
+        stage2_out(7, 0)
+        stage2_out(0, 1)
         stage2_mx(2, 1)
-        rank1(4, 1)
+        planes_inter(0, 0, 256, 512, "S")
         stage2_mx(3, 1)
-        stage2_out(2, 1)
-        rank1(5, 1)
+        stage2_out(1, 1)
+        planes_inter(1, 0, 0, 256, "S")
         stage2_mx(4, 1)
-        rank1(6, 1)
-        stage2_out(3, 1)
-        planes_inter(0, 1, 0, 256, "S")
+        stage2_out(2, 1)
+        planes_quant(0, 0, 0, 512)
         stage2_mx(5, 1)
+        rank1(4, 1)
+        planes_inter(1, 0, 256, 512, "S")
         planes_scales(0, 0)
+        stage2_out(3, 1)
+        rank1(5, 1)
+        rank1(6, 1)
+        planes_inter(0, 1, 0, 256, "S")
         stage2_out(4, 1)
-        planes_inter(0, 1, 256, 512, "S")
-        rank1(7, 1)
         planes_quant(1, 0, 0, 512)
-        stage2_mx(6, 1)
-        stage2_mx(7, 1)
         planes_scales(1, 0)
+        stage2_mx(6, 1)
         stage2_out(5, 1)
+        stage2_mx(7, 1)
+        rank1(7, 1)
         stage2_out(6, 1)
         stage2_out(7, 1)
+        planes_inter(0, 1, 256, 512, "S")
         planes_inter(1, 1, 0, 256, "V")
+        planes_inter(1, 1, 256, 512, "S")
         planes_quant(0, 1, 0, 512)
         planes_scales(0, 1)
         planes_quant(1, 1, 0, 256)
-        planes_inter(1, 1, 256, 512, "S")
         planes_quant(1, 1, 256, 512)
         planes_scales(1, 1)

@@ -56,7 +56,6 @@ def tile_girsanovreweightedneurallagcovariance_x2_kernel(
         bf = keep.tile([P, 8], F32)
         pf = keep.tile([P, 8], F32)
         bias_f = keep.tile([P, 8], F32)
-        nc.sync.dma_start(out=w_nat[:].bitcast(I32), in_=w_words[0].bitcast(I32))
         xr = {}
         for name, x in (("x0", x0), ("x1", x1)):
             for g in range(2):
@@ -65,7 +64,13 @@ def tile_girsanovreweightedneurallagcovariance_x2_kernel(
                 src = x[512 * g : 512 * g + 512, :].rearrange("(p j) d -> p j d", j=4)
                 for jp in range(2):
                     nc.sync.dma_start(out=t[:, 2 * jp : 2 * jp + 2, :], in_=src[:, 2 * jp : 2 * jp + 2, :])
+                    if (name, g, jp) == ("x0", 0, 0):
+                        nc.sync.dma_start(out=w_nat[:].bitcast(I32), in_=w_words[0].bitcast(I32))
 
+        a_bc = keep.tile([P, T], BF16)
+        b_bc = keep.tile([P, T], BF16)
+        nc.sync.dma_start(out=a_bc[:], in_=a.partition_broadcast(P))
+        nc.sync.dma_start(out=b_bc[:], in_=b.partition_broadcast(P))
         nc.gpsimd.tensor_tensor(out=pf[:], in0=a_h[:], in1=b_h[:], op=MUL)
         for t, v in ((bias_f, bias_h), (af, a_h), (bf, b_h)):
             nc.gpsimd.tensor_copy(out=t[:], in_=v[:])
@@ -73,14 +78,14 @@ def tile_girsanovreweightedneurallagcovariance_x2_kernel(
         w_perm = keep.tile([P, 2 * K], U8, align_bytes=64)
         ws_perm = keep.tile([P, K], U8, align_bytes=64)
 
-        def permute(g):
+        def permute(g, j0):
             nc.vector.tensor_copy(
-                out=w_perm[:, 1024 * g : 1024 * g + 1024].rearrange("p (j m b) -> p j m b", j=4, b=2),
-                in_=w_nat[:, 1024 * g : 1024 * g + 1024].rearrange("p (m j b) -> p j m b", j=4, b=2),
+                out=w_perm[:, 1024 * g + 256 * j0 : 1024 * g + 256 * j0 + 512].rearrange("p (j m b) -> p j m b", j=2, b=2),
+                in_=w_nat[:, 1024 * g : 1024 * g + 1024].rearrange("p (m j b) -> p j m b", j=4, b=2)[:, j0 : j0 + 2],
             )
             nc.vector.tensor_copy(
-                out=ws_perm[:, 512 * g : 512 * g + 512].rearrange("p (j m) -> p j m", j=4),
-                in_=ws_nat[:, 512 * g : 512 * g + 512].rearrange("p (m j) -> p j m", j=4),
+                out=ws_perm[:, 512 * g + 128 * j0 : 512 * g + 128 * j0 + 256].rearrange("p (j m) -> p j m", j=2),
+                in_=ws_nat[:, 512 * g : 512 * g + 512].rearrange("p (m j) -> p j m", j=4)[:, j0 : j0 + 2],
             )
 
         xq = {}
@@ -121,25 +126,31 @@ def tile_girsanovreweightedneurallagcovariance_x2_kernel(
             xs[name, g] = cs
 
         ct = {}
+        ybank = {}
 
-        def stage1(name, k, *groups):
-            if 0 in groups:
+        def stage1_mx(name, k, g):
+            bank = psum.tile([P, 512], F32, name="ps", bufs=BUFS["ps"])
+            ybank[name, k, g] = bank
+            nc.tensor.matmul_mx(
+                out=bank[:],
+                lhsT=w_perm[:, 256 * k : 256 * k + 256].bitcast(FP4X4),
+                lhsT_scale=ws_perm[:, 128 * k : 128 * k + 128],
+                rhs=xq[name, g][:].bitcast(FP8X4),
+                rhs_scale=xs[name, g][:],
+                start=True,
+                stop=True,
+            )
+
+        def stage1_act(name, k, g):
+            if g == 0:
                 ct[name, k] = work.tile([P, 1024], F32, name="ct_" + name, bufs=8 if name == "x1" else 4)
-            c = ct[name, k]
-            for g in groups:
-                mm = psum.tile([P, 512], F32, name="ps", bufs=BUFS["ps"])
-                nc.tensor.matmul_mx(
-                    out=mm[:],
-                    lhsT=w_perm[:, 256 * k : 256 * k + 256].bitcast(FP4X4),
-                    lhsT_scale=ws_perm[:, 128 * k : 128 * k + 128],
-                    rhs=xq[name, g][:].bitcast(FP8X4),
-                    rhs_scale=xs[name, g][:],
-                    start=True,
-                    stop=True,
-                )
-                nc.scalar.activation(
-                    out=c[:, 512 * g : 512 * g + 512], in_=mm[:], func=TANH, bias=bias_f[:, k : k + 1], scale=1.0
-                )
+            nc.scalar.activation(
+                out=ct[name, k][:, 512 * g : 512 * g + 512],
+                in_=ybank[name, k, g][:],
+                func=TANH,
+                bias=bias_f[:, k : k + 1],
+                scale=1.0,
+            )
 
         m0 = keep.tile([P, 8], F32)
         lq = [keep.tile([P, 1024], U32, name="lq_%d" % g, align_bytes=64) for g in range(2)]
@@ -148,32 +159,30 @@ def tile_girsanovreweightedneurallagcovariance_x2_kernel(
         rsc = [keep.tile([P, 1024], U8, name="rsc_%d" % g, align_bytes=64) for g in range(2)]
         p_bc = keep.tile([P, 1024], F32)
         rs = keep.tile([P, 1], F32)
-        nzr = keep.tile([P, 1], F32)
+        nz = keep.tile([P, 1], F32)
 
         def weights():
-            for h in range(2):
-                bank = psum.tile([P, 512], F32, name="ps", bufs=BUFS["ps"])
-                for j in range(4):
-                    nc.tensor.matmul(
-                        out=bank[:, 128 * j : 128 * j + 128],
-                        lhsT=pf[:, 4 * h + j : 4 * h + j + 1].to_broadcast([P, P]),
-                        rhs=ident[:],
-                        start=True,
-                        stop=True,
-                    )
-                nc.scalar.copy(out=p_bc[:, 512 * h : 512 * h + 512], in_=bank[:])
+            nc.gpsimd.tensor_tensor(
+                out=p_bc[:].rearrange("p (g j q) -> p g j q", g=2, j=4),
+                in0=a_bc[:].rearrange("p (g q j) -> p g j q", g=2, j=4),
+                in1=b_bc[:].rearrange("p (g q j) -> p g j q", g=2, j=4),
+                op=MUL,
+            )
 
-        def norm():
-            psum_col = keep.tile([P, 1], F32)
-            nc.vector.reduce_sum(out=psum_col[:], in_=pf[:], axis=AX)
-            small = psum.tile([P, 512], F32, name="ps", bufs=BUFS["ps"])
-            nc.tensor.matmul(out=small[:, 0:1], lhsT=ones[:], rhs=psum_col[:], start=True, stop=True)
+        nbank = {}
+
+        def norm_mm():
+            nbank[0] = psum.tile([P, 512], F32, name="ps", bufs=BUFS["ps"])
+            nc.tensor.matmul(out=nbank[0][:, 0:8], lhsT=ones[:], rhs=pf[:], start=True, stop=True)
+
+        def norm_take():
+            p_sums = keep.tile([P, 8], F32)
             z = keep.tile([P, 1], F32)
-            nc.vector.tensor_copy(out=z[:], in_=small[:, 0:1])
+            nc.scalar.activation(out=p_sums[:], in_=nbank[0][:, 0:8], func=COPY, accum_out=z[:])
             nc.gpsimd.tensor_tensor(out=rs[:], in0=z[:], in1=neg_half[:], op=mybir.AluOpType.pow)
             rs2 = keep.tile([P, 1], F32)
             nc.gpsimd.tensor_tensor(out=rs2[:], in0=rs[:], in1=rs[:], op=MUL)
-            nc.gpsimd.tensor_scalar(out=nzr[:], in0=rs2[:], scalar1=rs[:, 0:1], scalar2=-1.0, op0=MUL, op1=MUL)
+            nc.gpsimd.tensor_scalar(out=nz[:], in0=rs2[:], scalar1=-1.0, scalar2=0.0, op0=MUL, op1=ADD)
 
         def c0_m(k):
             junk = work.tile([P, 1024], BF16, name="junk", bufs=2)
@@ -212,18 +221,23 @@ def tile_girsanovreweightedneurallagcovariance_x2_kernel(
 
         rf = {}
 
-        def c1_unit(quad, g, j):
+        c1_bank = {}
+
+        def c1_tr(quad, g, j):
+            bank = psum.tile([P, 512], F32, name="ps", bufs=BUFS["ps"])
+            c1_bank[quad, g, j] = bank
+            col = 512 * g + 128 * j
+            for f in range(4):
+                nc.tensor.transpose(
+                    bank[:, 128 * f : 128 * f + 128], ct["x1", 4 * quad + f][:, col : col + 128], ident[:]
+                )
+
+        def c1_evac(quad, g, j):
             if j == 0:
                 rf[quad, g] = work.tile([P, 4, 512], F32, name="rf", bufs=3)
-            bank = psum.tile([P, 512], F32, name="ps", bufs=BUFS["ps"])
-            col = 512 * g + 128 * j
-            for jf in range(4):
-                nc.tensor.transpose(
-                    bank[:, 128 * jf : 128 * jf + 128], ct["x1", 4 * quad + jf][:, col : col + 128], ident[:]
-                )
             nc.scalar.activation(
                 out=rf[quad, g][:, j, :].rearrange("p (q f) -> p q f", f=4),
-                in_=bank[:].rearrange("p (f q) -> p q f", f=4),
+                in_=c1_bank[quad, g, j][:].rearrange("p (f q) -> p q f", f=4),
                 func=COPY,
                 scale=bf[:, 4 * g + j : 4 * g + j + 1],
             )
@@ -253,7 +267,9 @@ def tile_girsanovreweightedneurallagcovariance_x2_kernel(
             )
 
         def m1_take(quad):
-            nc.scalar.copy(out=m1_bc[:, 512 * quad : 512 * quad + 512], in_=acc[quad][:])
+            nc.scalar.activation(
+                out=m1_bc[:, 512 * quad : 512 * quad + 512], in_=acc[quad][:], func=COPY, scale=nz[:, 0:1]
+            )
 
         m1 = keep.tile([P, 8], F32)
 
@@ -270,6 +286,8 @@ def tile_girsanovreweightedneurallagcovariance_x2_kernel(
                 in_=rbf[quad, g][:],
             )
 
+        spread = {}
+
         def m1_spread(quad):
             bank = psum.tile([P, 512], F32, name="ps", bufs=BUFS["ps"])
             for f in range(4):
@@ -280,21 +298,17 @@ def tile_girsanovreweightedneurallagcovariance_x2_kernel(
                     start=True,
                     stop=True,
                 )
-            nc.scalar.copy(
+            spread[quad] = bank
+
+        def m1_unspread(quad):
+            nc.scalar.activation(
                 out=m1_bc[:, 512 * quad : 512 * quad + 512].rearrange("p (q f) -> p q f", f=4),
-                in_=bank[:].rearrange("p (f q) -> p q f", f=4),
+                in_=spread[quad][:].rearrange("p (f q) -> p q f", f=4),
+                func=COPY,
+                scale=nz[:, 0:1],
             )
 
         res = {}
-        gm = {}
-
-        def rank1(k, h):
-            t = work.tile([P, 512], F32, name="gm", bufs=8)
-            gm[k, h] = t
-            nc.gpsimd.tensor_scalar(
-                out=t[:], in0=m1_bc[:, 512 * h : 512 * h + 512], scalar1=m0[:, k : k + 1], scalar2=nzr[:, 0:1], op0=MUL, op1=MUL
-            )
-
         s_bank = {}
 
         def stage2_mx(k, h):
@@ -316,11 +330,28 @@ def tile_girsanovreweightedneurallagcovariance_x2_kernel(
             if j == 0:
                 res[quad, h] = work.tile([P, 4, 512], F32, name="res", bufs=4)
             nc.vector.scalar_tensor_tensor(
-                out=res[quad, h][:, j, :], in0=s_bank[k, h][:], scalar=rs[:, 0:1], in1=gm[k, h][:], op0=MUL, op1=ADD
+                out=res[quad, h][:, j, :],
+                in0=m1_bc[:, 512 * h : 512 * h + 512],
+                scalar=m0[:, k : k + 1],
+                in1=s_bank[k, h][:],
+                op0=MUL,
+                op1=ADD,
             )
+
+        def scale_out(k, h, eng):
+            quad, j = divmod(k, 4)
+            r = work.tile([P, 512], F32, name="r", bufs=8)
+            if eng == "P":
+                nc.gpsimd.tensor_scalar(
+                    out=r[:], in0=res[quad, h][:, j, :], scalar1=rs[:, 0:1], scalar2=0.0, op0=MUL, op1=ADD
+                )
+            elif eng == "S":
+                nc.scalar.activation(out=r[:], in_=res[quad, h][:, j, :], func=COPY, scale=rs[:, 0:1])
+            else:
+                nc.vector.tensor_scalar(out=r[:], in0=res[quad, h][:, j, :], scalar1=rs[:, 0:1], scalar2=None, op0=MUL)
             nc.sync.dma_start(
                 out=out_0[512 * quad : 512 * quad + 512, :].rearrange("(p j) n -> p j n", j=4)[:, j, 512 * h : 512 * h + 512],
-                in_=res[quad, h][:, j, :],
+                in_=r[:],
             )
 
         ybf = {}
@@ -332,9 +363,11 @@ def tile_girsanovreweightedneurallagcovariance_x2_kernel(
             dst = ybf[quad, h][:, 4 * c0 : 4 * c1].rearrange("p (c i j) -> p c j i", i=4, j=4)
             srcv = res[quad, h][:, :, c0:c1].rearrange("p j (c i) -> p c j i", i=4)
             if eng == "S":
-                nc.scalar.copy(out=dst, in_=srcv)
+                nc.scalar.activation(out=dst, in_=srcv, func=COPY, scale=rs[:, 0:1])
+            elif eng == "P":
+                nc.gpsimd.tensor_scalar(out=dst, in0=srcv, scalar1=rs[:, 0:1], scalar2=0.0, op0=MUL, op1=ADD)
             else:
-                nc.vector.tensor_copy(out=dst, in_=srcv)
+                nc.vector.tensor_scalar(out=dst, in0=srcv, scalar1=rs[:, 0:1], scalar2=None, op0=MUL)
 
         def planes_quant(quad, h, c0, c1):
             if (quad, h) not in yq:
@@ -359,210 +392,262 @@ def tile_girsanovreweightedneurallagcovariance_x2_kernel(
                     in_=scales[32 * q : 32 * q + 4, :].bitcast(I32),
                 )
 
-        permute(0)
-        weights()
         x_tr("x0", 0, (0,))
-        permute(1)
-        x_evac("x0", 0, 0, "S")
         x_tr("x0", 0, (1,))
         x_tr("x0", 1, (0,))
-        x_evac("x0", 0, 1, "S")
-        norm()
+        x_evac("x0", 0, 0, "S")
         x_tr("x0", 1, (1,))
-        x_evac("x0", 1, 0, "V")
-        x_evac("x0", 1, 1, "S")
         x_tr("x1", 0, (0,))
+        weights()
+        x_evac("x0", 0, 1, "V")
         x_tr("x1", 0, (1,))
+        x_evac("x0", 1, 0, "S")
+        x_evac("x0", 1, 1, "S")
         x_tr("x1", 1, (0,))
+        permute(0, 0)
         x_quant("x0", 0)
-        x_quant("x0", 1)
+        permute(0, 2)
         x_evac("x1", 0, 0, "S")
-        x_evac("x1", 0, 1, "S")
-        x_evac("x1", 1, 0, "S")
-        stage1("x0", 0, 0)
+        x_quant("x0", 1)
+        x_evac("x1", 0, 1, "V")
+        permute(1, 0)
         x_tr("x1", 1, (1,))
-        stage1("x0", 0, 1)
-        stage1("x0", 1, 0)
-        stage1("x0", 1, 1)
-        c0_tr(0, 0)
         x_quant("x1", 0)
-        x_evac("x1", 1, 1, "V")
-        stage1("x0", 2, 0)
-        stage1("x0", 2, 1)
+        x_evac("x1", 1, 0, "S")
+        x_evac("x1", 1, 1, "S")
+        stage1_mx("x0", 0, 0)
+        stage1_mx("x0", 0, 1)
         x_quant("x1", 1)
-        stage1("x1", 0, 0)
+        stage1_mx("x0", 1, 0)
+        stage1_mx("x0", 1, 1)
+        stage1_mx("x0", 2, 0)
+        permute(1, 2)
+        stage1_mx("x0", 2, 1)
+        stage1_act("x0", 0, 0)
+        c0_tr(0, 0)
+        stage1_mx("x0", 3, 0)
+        stage1_act("x0", 0, 1)
+        c0_evac(0, 0)
+        stage1_act("x0", 1, 0)
+        stage1_mx("x0", 3, 1)
+        stage1_act("x0", 1, 1)
         c0_m(0)
         c0_tr(0, 1)
-        c0_evac(0, 0)
-        c0_tr(1, 0)
-        stage1("x1", 0, 1)
+        stage1_act("x0", 2, 0)
         c0_evac(0, 1)
-        stage1("x1", 1, 0)
-        stage1("x1", 1, 1)
-        c0_evac(1, 0)
-        c0_tr(1, 1)
-        c0_tr(2, 0)
-        stage1("x1", 2, 0)
+        stage1_act("x0", 2, 1)
+        stage1_act("x0", 3, 0)
+        c0_tr(1, 0)
+        stage1_act("x0", 3, 1)
         c0_m(1)
-        stage1("x0", 3, 0)
-        stage1("x0", 3, 1)
+        c0_evac(1, 0)
+        stage1_mx("x1", 0, 0)
+        stage1_mx("x1", 0, 1)
+        stage1_act("x1", 0, 0)
+        c0_tr(1, 1)
+        stage1_mx("x1", 1, 0)
+        stage1_act("x1", 0, 1)
         c0_evac(1, 1)
-        stage1("x1", 2, 1)
-        c0_tr(2, 1)
-        c0_evac(2, 0)
+        stage1_mx("x1", 1, 1)
         c0_m(2)
-        stage1("x1", 3, 0)
-        c0_quant(0, 0)
-        stage1("x0", 4, 0)
-        c0_tr(3, 0)
-        stage1("x1", 3, 1)
-        c0_evac(2, 1)
-        stage1("x0", 4, 1)
-        c0_tr(3, 1)
-        c1_unit(0, 0, 0)
-        stage1("x1", 4, 0)
-        c0_evac(3, 0)
-        stage1("x1", 4, 1)
-        c0_quant(0, 1)
-        c0_tr(4, 0)
-        c1_unit(0, 0, 1)
-        c0_evac(3, 1)
-        c1_unit(0, 0, 2)
-        c1_sum(0, 0, 0)
+        stage1_mx("x1", 2, 0)
+        stage1_act("x1", 1, 0)
+        c0_tr(2, 0)
+        stage1_mx("x1", 2, 1)
+        stage1_act("x1", 1, 1)
+        c0_evac(2, 0)
+        stage1_mx("x1", 3, 0)
+        stage1_mx("x1", 3, 1)
+        stage1_act("x1", 2, 0)
+        c0_tr(2, 1)
         c0_m(3)
-        c0_evac(4, 0)
-        c1_unit(0, 0, 3)
+        stage1_act("x1", 2, 1)
+        c0_evac(2, 1)
+        stage1_act("x1", 3, 0)
+        c0_tr(3, 0)
+        stage1_mx("x0", 4, 0)
+        c0_evac(3, 0)
+        stage1_act("x1", 3, 1)
+        stage1_mx("x0", 4, 1)
+        c0_tr(3, 1)
+        stage1_mx("x0", 5, 0)
+        c0_evac(3, 1)
+        stage1_mx("x0", 5, 1)
+        stage1_mx("x0", 6, 0)
+        stage1_act("x0", 4, 0)
+        stage1_mx("x0", 6, 1)
+        stage1_act("x0", 4, 1)
+        stage1_act("x0", 5, 0)
+        stage1_act("x0", 5, 1)
+        c0_tr(4, 0)
+        stage1_mx("x0", 7, 0)
+        stage1_act("x0", 6, 0)
+        stage1_act("x0", 6, 1)
+        c0_quant(0, 0)
         c0_m(4)
-        c1_m(4)
-        stage1("x0", 5, 0)
+        stage1_act("x0", 7, 0)
+        stage1_mx("x0", 7, 1)
         c0_tr(4, 1)
-        stage1("x1", 5, 0)
-        c0_quant(1, 0)
-        stage1("x0", 5, 1)
-        stage1("x0", 6, 0)
-        stage1("x1", 5, 1)
-        c0_evac(4, 1)
-        c1_inter(0, 0)
-        c0_m(5)
-        stage1("x1", 6, 0)
+        c0_evac(4, 0)
+        stage1_act("x0", 7, 1)
+        stage1_mx("x1", 4, 0)
+        stage1_mx("x1", 4, 1)
+        c1_tr(0, 0, 0)
+        c0_quant(0, 1)
+        stage1_act("x1", 4, 0)
         c0_tr(5, 0)
-        c1_unit(0, 1, 0)
+        stage1_mx("x1", 5, 0)
+        c0_evac(4, 1)
+        c0_m(5)
+        stage1_act("x1", 4, 1)
+        stage1_mx("x1", 5, 1)
+        c1_evac(0, 0, 0)
+        stage1_act("x1", 5, 0)
+        stage1_mx("x1", 6, 0)
+        c1_tr(0, 0, 1)
         c0_tr(5, 1)
-        c1_unit(0, 1, 1)
-        c1_unit(0, 1, 2)
-        c1_sum(0, 0, 1)
+        stage1_act("x1", 5, 1)
         c0_evac(5, 0)
-        c1_unit(0, 1, 3)
-        stage1("x1", 6, 1)
-        stage1("x0", 6, 1)
-        c0_quant(1, 1)
-        stage1("x0", 7, 0)
-        c0_evac(5, 1)
-        c1_m(5)
-        stage1("x0", 7, 1)
-        stage1("x1", 7, 0)
-        stage1("x1", 7, 1)
-        c0_quant(2, 0)
-        c1_quant(0, 0)
-        c0_tr(6, 0)
-        c1_sum(0, 0, 2)
-        c1_sum(0, 0, 3)
-        c1_m(6)
+        c0_quant(1, 0)
+        stage1_mx("x1", 6, 1)
+        stage1_act("x1", 6, 0)
+        c1_evac(0, 0, 1)
         c0_m(6)
-        c1_sum(0, 1, 0)
-        c0_evac(6, 0)
+        stage1_mx("x1", 7, 0)
+        c1_sum(0, 0, 0)
+        stage1_act("x1", 6, 1)
+        c0_tr(6, 0)
+        c1_tr(0, 0, 2)
+        stage1_mx("x1", 7, 1)
+        c0_evac(5, 1)
+        stage1_act("x1", 7, 0)
+        c0_quant(1, 1)
+        c1_evac(0, 0, 2)
+        stage1_act("x1", 7, 1)
         c0_tr(6, 1)
-        c1_unit(1, 0, 0)
-        c1_unit(1, 0, 1)
-        c1_unit(1, 0, 2)
-        c1_sum(0, 1, 1)
-        c0_quant(2, 1)
         c0_m(7)
-        c1_inter(0, 1)
-        c1_unit(1, 0, 3)
+        c1_tr(0, 0, 3)
+        c0_evac(6, 0)
+        c1_m(4)
+        c1_sum(0, 0, 1)
+        c1_evac(0, 0, 3)
+        c0_quant(2, 0)
         c0_tr(7, 0)
-        c1_unit(1, 1, 0)
-        c1_sum(0, 1, 2)
-        c1_sum(0, 1, 3)
-        m1_take(0)
-        rank1(0, 0)
-        c1_m(7)
         c0_evac(6, 1)
-        rank1(1, 0)
-        rank1(2, 0)
+        c1_tr(0, 1, 0)
+        c1_m(5)
+        c1_evac(0, 1, 0)
         c0_tr(7, 1)
-        c1_unit(1, 1, 1)
+        c1_m(6)
         c0_evac(7, 0)
-        c1_unit(1, 1, 2)
-        c1_inter(1, 0)
-        c1_quant(0, 1)
-        rank1(3, 0)
-        c0_quant(3, 0)
-        c1_unit(1, 1, 3)
+        c0_quant(2, 1)
+        c1_tr(0, 1, 1)
+        norm_mm()
+        c1_sum(0, 0, 2)
+        c1_evac(0, 1, 1)
+        c1_m(7)
         c0_evac(7, 1)
-        stage2_mx(0, 0)
-        c1_quant(1, 0)
-        stage2_mx(1, 0)
-        stage2_mx(2, 0)
-        m1_spread(1)
-        rank1(4, 0)
-        stage2_mx(3, 0)
+        c1_tr(0, 1, 2)
+        c0_quant(3, 0)
+        c1_evac(0, 1, 2)
+        c1_sum(0, 0, 3)
+        c1_tr(0, 1, 3)
         c0_quant(3, 1)
-        stage2_out(0, 0)
-        stage2_mx(4, 0)
-        stage2_mx(5, 0)
-        stage2_out(1, 0)
+        c1_evac(0, 1, 3)
+        norm_take()
+        c1_sum(0, 1, 0)
+        c1_tr(1, 0, 0)
+        c1_tr(1, 0, 1)
+        c1_tr(1, 0, 2)
+        c1_tr(1, 0, 3)
+        c1_inter(0, 0)
+        c1_inter(0, 1)
+        c1_tr(1, 1, 0)
+        c1_sum(0, 1, 1)
+        c1_tr(1, 1, 1)
+        c1_quant(0, 0)
+        c1_tr(1, 1, 2)
+        c1_quant(0, 1)
+        c1_evac(1, 0, 0)
+        c1_tr(1, 1, 3)
+        c1_evac(1, 0, 1)
+        c1_evac(1, 0, 2)
+        c1_evac(1, 0, 3)
+        c1_sum(0, 1, 2)
+        c1_evac(1, 1, 0)
+        c1_evac(1, 1, 1)
+        c1_evac(1, 1, 2)
+        c1_evac(1, 1, 3)
+        c1_inter(1, 0)
+        c1_sum(0, 1, 3)
+        stage2_mx(0, 0)
+        m1_take(0)
         c1_inter(1, 1)
-        stage2_out(2, 0)
+        stage2_mx(1, 0)
+        stage2_out(0, 0)
+        stage2_mx(2, 0)
+        stage2_mx(3, 0)
+        stage2_mx(4, 0)
+        stage2_out(1, 0)
+        stage2_mx(5, 0)
         stage2_mx(6, 0)
-        stage2_out(3, 0)
         stage2_mx(7, 0)
+        stage2_out(2, 0)
+        stage2_out(3, 0)
         stage2_out(4, 0)
-        rank1(5, 0)
+        c1_quant(1, 0)
         c1_quant(1, 1)
-        rank1(6, 0)
-        rank1(7, 0)
         stage2_out(5, 0)
-        rank1(0, 1)
-        rank1(1, 1)
-        stage2_mx(0, 1)
-        stage2_out(6, 0)
+        scale_out(0, 0, "P")
         planes_inter(0, 0, 0, 256, "S")
-        stage2_mx(1, 1)
-        rank1(2, 1)
-        rank1(3, 1)
-        stage2_out(7, 0)
-        stage2_out(0, 1)
-        stage2_mx(2, 1)
+        scale_out(1, 0, "P")
+        scale_out(2, 0, "P")
         planes_inter(0, 0, 256, 512, "S")
-        stage2_mx(3, 1)
-        stage2_out(1, 1)
-        planes_inter(1, 0, 0, 256, "S")
-        stage2_mx(4, 1)
-        stage2_out(2, 1)
+        stage2_out(6, 0)
+        scale_out(3, 0, "P")
+        scale_out(4, 0, "P")
+        scale_out(5, 0, "P")
+        stage2_out(7, 0)
+        scale_out(6, 0, "P")
         planes_quant(0, 0, 0, 512)
+        scale_out(7, 0, "P")
+        m1_spread(1)
+        stage2_mx(0, 1)
+        stage2_mx(1, 1)
+        stage2_mx(2, 1)
+        stage2_mx(3, 1)
+        m1_unspread(1)
+        stage2_mx(4, 1)
         stage2_mx(5, 1)
-        rank1(4, 1)
-        planes_inter(1, 0, 256, 512, "S")
         planes_scales(0, 0)
-        stage2_out(3, 1)
-        rank1(5, 1)
-        rank1(6, 1)
-        planes_inter(0, 1, 0, 256, "S")
-        stage2_out(4, 1)
-        planes_quant(1, 0, 0, 512)
-        planes_scales(1, 0)
+        stage2_out(0, 1)
+        scale_out(0, 1, "P")
+        stage2_out(1, 1)
         stage2_mx(6, 1)
-        stage2_out(5, 1)
+        scale_out(1, 1, "P")
+        stage2_out(2, 1)
+        planes_inter(1, 0, 0, 256, "S")
         stage2_mx(7, 1)
-        rank1(7, 1)
+        stage2_out(3, 1)
+        scale_out(2, 1, "P")
+        stage2_out(4, 1)
+        planes_inter(1, 0, 256, 512, "S")
+        planes_quant(1, 0, 0, 512)
+        stage2_out(5, 1)
+        planes_scales(1, 0)
+        scale_out(3, 1, "P")
         stage2_out(6, 1)
         stage2_out(7, 1)
+        scale_out(4, 1, "P")
+        scale_out(5, 1, "P")
+        planes_inter(0, 1, 0, 256, "S")
         planes_inter(0, 1, 256, 512, "S")
+        scale_out(6, 1, "V")
+        scale_out(7, 1, "P")
         planes_inter(1, 1, 0, 256, "V")
-        planes_inter(1, 1, 256, 512, "S")
         planes_quant(0, 1, 0, 512)
         planes_scales(0, 1)
         planes_quant(1, 1, 0, 256)
+        planes_inter(1, 1, 256, 512, "S")
         planes_quant(1, 1, 256, 512)
         planes_scales(1, 1)

@@ -67,10 +67,6 @@ def tile_girsanovreweightedneurallagcovariance_x2_kernel(
                     if (name, g, jp) == ("x0", 0, 0):
                         nc.sync.dma_start(out=w_nat[:].bitcast(I32), in_=w_words[0].bitcast(I32))
 
-        a_bc = keep.tile([P, T], BF16)
-        b_bc = keep.tile([P, T], BF16)
-        nc.sync.dma_start(out=a_bc[:], in_=a.partition_broadcast(P))
-        nc.sync.dma_start(out=b_bc[:], in_=b.partition_broadcast(P))
         nc.gpsimd.tensor_tensor(out=pf[:], in0=a_h[:], in1=b_h[:], op=MUL)
         for t, v in ((bias_f, bias_h), (af, a_h), (bf, b_h)):
             nc.gpsimd.tensor_copy(out=t[:], in_=v[:])
@@ -161,13 +157,22 @@ def tile_girsanovreweightedneurallagcovariance_x2_kernel(
         rs = keep.tile([P, 1], F32)
         nz = keep.tile([P, 1], F32)
 
-        def weights():
-            nc.gpsimd.tensor_tensor(
-                out=p_bc[:].rearrange("p (g j q) -> p g j q", g=2, j=4),
-                in0=a_bc[:].rearrange("p (g q j) -> p g j q", g=2, j=4),
-                in1=b_bc[:].rearrange("p (g q j) -> p g j q", g=2, j=4),
-                op=MUL,
-            )
+        wbank = {}
+
+        def weights_mm(h):
+            bank = psum.tile([P, 512], F32, name="ps", bufs=BUFS["ps"])
+            wbank[h] = bank
+            for j in range(4):
+                nc.tensor.matmul(
+                    out=bank[:, 128 * j : 128 * j + 128],
+                    lhsT=pf[:, 4 * h + j : 4 * h + j + 1].to_broadcast([P, P]),
+                    rhs=ident[:],
+                    start=True,
+                    stop=True,
+                )
+
+        def weights_take(h):
+            nc.scalar.copy(out=p_bc[:, 512 * h : 512 * h + 512], in_=wbank[h][:])
 
         nbank = {}
 
@@ -182,7 +187,7 @@ def tile_girsanovreweightedneurallagcovariance_x2_kernel(
             nc.gpsimd.tensor_tensor(out=rs[:], in0=z[:], in1=neg_half[:], op=mybir.AluOpType.pow)
             rs2 = keep.tile([P, 1], F32)
             nc.gpsimd.tensor_tensor(out=rs2[:], in0=rs[:], in1=rs[:], op=MUL)
-            nc.gpsimd.tensor_scalar(out=nz[:], in0=rs2[:], scalar1=-1.0, scalar2=0.0, op0=MUL, op1=ADD)
+            nc.gpsimd.tensor_scalar(out=nz[:], in0=rs2[:], scalar1=rs[:, 0:1], scalar2=-1.0, op0=MUL, op1=MUL)
 
         def c0_m(k):
             junk = work.tile([P, 1024], BF16, name="junk", bufs=2)
@@ -330,29 +335,26 @@ def tile_girsanovreweightedneurallagcovariance_x2_kernel(
             if j == 0:
                 res[quad, h] = work.tile([P, 4, 512], F32, name="res", bufs=4)
             nc.vector.scalar_tensor_tensor(
-                out=res[quad, h][:, j, :],
-                in0=m1_bc[:, 512 * h : 512 * h + 512],
-                scalar=m0[:, k : k + 1],
-                in1=s_bank[k, h][:],
-                op0=MUL,
-                op1=ADD,
+                out=res[quad, h][:, j, :], in0=s_bank[k, h][:], scalar=rs[:, 0:1], in1=gm[k, h][:], op0=MUL, op1=ADD
             )
-
-        def scale_out(k, h, eng):
-            quad, j = divmod(k, 4)
-            r = work.tile([P, 512], F32, name="r", bufs=8)
-            if eng == "P":
-                nc.gpsimd.tensor_scalar(
-                    out=r[:], in0=res[quad, h][:, j, :], scalar1=rs[:, 0:1], scalar2=0.0, op0=MUL, op1=ADD
-                )
-            elif eng == "S":
-                nc.scalar.activation(out=r[:], in_=res[quad, h][:, j, :], func=COPY, scale=rs[:, 0:1])
-            else:
-                nc.vector.tensor_scalar(out=r[:], in0=res[quad, h][:, j, :], scalar1=rs[:, 0:1], scalar2=None, op0=MUL)
             nc.sync.dma_start(
                 out=out_0[512 * quad : 512 * quad + 512, :].rearrange("(p j) n -> p j n", j=4)[:, j, 512 * h : 512 * h + 512],
-                in_=r[:],
+                in_=res[quad, h][:, j, :],
             )
+
+        gm = {}
+
+        def rank1(k, h, eng):
+            gm[k, h] = work.tile([P, 512], F32, name="gm", bufs=8)
+            row = m1_bc[:, 512 * h : 512 * h + 512]
+            if eng == "S":
+                nc.scalar.activation(out=gm[k, h][:], in_=row, func=COPY, scale=m0[:, k : k + 1])
+            elif eng == "P":
+                nc.gpsimd.tensor_scalar(
+                    out=gm[k, h][:], in0=row, scalar1=m0[:, k : k + 1], scalar2=0.0, op0=MUL, op1=ADD
+                )
+            else:
+                nc.vector.tensor_scalar(out=gm[k, h][:], in0=row, scalar1=m0[:, k : k + 1], scalar2=None, op0=MUL)
 
         ybf = {}
         yq = {}
@@ -363,17 +365,15 @@ def tile_girsanovreweightedneurallagcovariance_x2_kernel(
             dst = ybf[quad, h][:, 4 * c0 : 4 * c1].rearrange("p (c i j) -> p c j i", i=4, j=4)
             srcv = res[quad, h][:, :, c0:c1].rearrange("p j (c i) -> p c j i", i=4)
             if eng == "S":
-                nc.scalar.activation(out=dst, in_=srcv, func=COPY, scale=rs[:, 0:1])
-            elif eng == "P":
-                nc.gpsimd.tensor_scalar(out=dst, in0=srcv, scalar1=rs[:, 0:1], scalar2=0.0, op0=MUL, op1=ADD)
+                nc.scalar.copy(out=dst, in_=srcv)
             else:
-                nc.vector.tensor_scalar(out=dst, in0=srcv, scalar1=rs[:, 0:1], scalar2=None, op0=MUL)
+                nc.vector.tensor_copy(out=dst, in_=srcv)
 
         def planes_quant(quad, h, c0, c1):
             if (quad, h) not in yq:
                 yq[quad, h] = (
-                    work.tile([P, 512], U32, name="yq", bufs=2, align_bytes=64),
-                    work.tile([P, 512], U8, name="ys", bufs=2, align_bytes=64),
+                    work.tile([P, 512], U32, name="yq", bufs=4, align_bytes=64),
+                    work.tile([P, 512], U8, name="ys", bufs=4, align_bytes=64),
                 )
             codes, scales = yq[quad, h]
             nc.vector.quantize_mx(
@@ -392,262 +392,270 @@ def tile_girsanovreweightedneurallagcovariance_x2_kernel(
                     in_=scales[32 * q : 32 * q + 4, :].bitcast(I32),
                 )
 
+        warm_in = keep.tile([P, 512], BF16)
+        nc.vector.memset(warm_in[:], 0.0)
+        warm = psum.tile([P, 512], F32, name="acc", bufs=BUFS["acc"])
+        for i in range(6):
+            nc.tensor.matmul(out=warm[:], lhsT=warm_in[:, 0:P], rhs=warm_in[:], start=True, stop=True)
         x_tr("x0", 0, (0,))
         x_tr("x0", 0, (1,))
         x_tr("x0", 1, (0,))
-        x_evac("x0", 0, 0, "S")
         x_tr("x0", 1, (1,))
+        x_evac("x0", 0, 0, "S")
+        permute(0, 0)
         x_tr("x1", 0, (0,))
-        weights()
-        x_evac("x0", 0, 1, "V")
         x_tr("x1", 0, (1,))
         x_evac("x0", 1, 0, "S")
         x_evac("x0", 1, 1, "S")
-        x_tr("x1", 1, (0,))
-        permute(0, 0)
-        x_quant("x0", 0)
-        permute(0, 2)
+        x_evac("x0", 0, 1, "V")
         x_evac("x1", 0, 0, "S")
+        x_quant("x0", 0)
+        stage1_mx("x0", 0, 0)
+        weights_mm(0)
+        weights_mm(1)
+        permute(0, 2)
+        x_tr("x1", 1, (0,))
         x_quant("x0", 1)
         x_evac("x1", 0, 1, "V")
-        permute(1, 0)
-        x_tr("x1", 1, (1,))
-        x_quant("x1", 0)
-        x_evac("x1", 1, 0, "S")
-        x_evac("x1", 1, 1, "S")
-        stage1_mx("x0", 0, 0)
         stage1_mx("x0", 0, 1)
-        x_quant("x1", 1)
+        permute(1, 0)
         stage1_mx("x0", 1, 0)
-        stage1_mx("x0", 1, 1)
-        stage1_mx("x0", 2, 0)
-        permute(1, 2)
-        stage1_mx("x0", 2, 1)
+        x_quant("x1", 0)
         stage1_act("x0", 0, 0)
+        weights_take(0)
+        norm_mm()
+        x_tr("x1", 1, (1,))
+        weights_take(1)
+        stage1_mx("x0", 1, 1)
+        x_evac("x1", 1, 0, "V")
         c0_tr(0, 0)
-        stage1_mx("x0", 3, 0)
         stage1_act("x0", 0, 1)
-        c0_evac(0, 0)
-        stage1_act("x0", 1, 0)
-        stage1_mx("x0", 3, 1)
-        stage1_act("x0", 1, 1)
-        c0_m(0)
         c0_tr(0, 1)
+        permute(1, 2)
+        stage1_mx("x0", 2, 0)
+        stage1_act("x0", 1, 0)
+        c0_m(0)
+        x_evac("x1", 1, 1, "S")
+        stage1_mx("x0", 2, 1)
+        norm_take()
+        stage1_mx("x0", 3, 0)
+        stage1_act("x0", 1, 1)
+        stage1_mx("x0", 3, 1)
         stage1_act("x0", 2, 0)
-        c0_evac(0, 1)
-        stage1_act("x0", 2, 1)
-        stage1_act("x0", 3, 0)
         c0_tr(1, 0)
+        c0_evac(0, 0)
+        stage1_act("x0", 2, 1)
+        c0_evac(0, 1)
+        stage1_act("x0", 3, 0)
+        c0_tr(1, 1)
         stage1_act("x0", 3, 1)
-        c0_m(1)
-        c0_evac(1, 0)
+        x_quant("x1", 1)
+        c0_tr(2, 0)
         stage1_mx("x1", 0, 0)
         stage1_mx("x1", 0, 1)
-        stage1_act("x1", 0, 0)
-        c0_tr(1, 1)
-        stage1_mx("x1", 1, 0)
-        stage1_act("x1", 0, 1)
-        c0_evac(1, 1)
-        stage1_mx("x1", 1, 1)
-        c0_m(2)
-        stage1_mx("x1", 2, 0)
-        stage1_act("x1", 1, 0)
-        c0_tr(2, 0)
-        stage1_mx("x1", 2, 1)
-        stage1_act("x1", 1, 1)
-        c0_evac(2, 0)
-        stage1_mx("x1", 3, 0)
-        stage1_mx("x1", 3, 1)
-        stage1_act("x1", 2, 0)
         c0_tr(2, 1)
-        c0_m(3)
-        stage1_act("x1", 2, 1)
-        c0_evac(2, 1)
-        stage1_act("x1", 3, 0)
-        c0_tr(3, 0)
+        stage1_act("x1", 0, 0)
+        c0_evac(1, 0)
+        c0_evac(1, 1)
+        stage1_mx("x1", 1, 0)
         stage1_mx("x0", 4, 0)
-        c0_evac(3, 0)
-        stage1_act("x1", 3, 1)
+        c0_tr(3, 0)
+        c0_evac(2, 0)
+        stage1_act("x1", 0, 1)
+        c0_m(1)
+        c0_evac(2, 1)
         stage1_mx("x0", 4, 1)
-        c0_tr(3, 1)
-        stage1_mx("x0", 5, 0)
-        c0_evac(3, 1)
-        stage1_mx("x0", 5, 1)
-        stage1_mx("x0", 6, 0)
-        stage1_act("x0", 4, 0)
-        stage1_mx("x0", 6, 1)
-        stage1_act("x0", 4, 1)
-        stage1_act("x0", 5, 0)
-        stage1_act("x0", 5, 1)
-        c0_tr(4, 0)
-        stage1_mx("x0", 7, 0)
-        stage1_act("x0", 6, 0)
-        stage1_act("x0", 6, 1)
+        stage1_mx("x1", 1, 1)
+        c0_evac(3, 0)
         c0_quant(0, 0)
-        c0_m(4)
-        stage1_act("x0", 7, 0)
-        stage1_mx("x0", 7, 1)
-        c0_tr(4, 1)
+        c0_tr(3, 1)
+        c0_quant(0, 1)
+        stage1_act("x1", 1, 0)
+        stage1_mx("x0", 5, 0)
+        stage1_act("x0", 4, 0)
+        c0_evac(3, 1)
+        stage1_mx("x1", 2, 0)
+        stage1_mx("x0", 5, 1)
+        stage1_act("x0", 4, 1)
+        c0_m(2)
+        stage1_act("x1", 1, 1)
+        stage1_mx("x1", 2, 1)
+        stage1_mx("x0", 6, 0)
+        c0_tr(4, 0)
+        stage1_act("x0", 5, 0)
+        stage1_act("x1", 2, 0)
+        stage1_mx("x0", 6, 1)
         c0_evac(4, 0)
+        stage1_act("x0", 5, 1)
+        stage1_mx("x1", 3, 0)
+        c0_tr(4, 1)
+        c0_m(3)
+        c0_quant(1, 0)
+        stage1_mx("x0", 7, 0)
+        stage1_act("x1", 2, 1)
+        stage1_act("x0", 6, 0)
+        c0_evac(4, 1)
+        c0_tr(5, 0)
+        stage1_mx("x1", 3, 1)
+        stage1_mx("x0", 7, 1)
+        stage1_act("x0", 6, 1)
+        stage1_act("x1", 3, 0)
+        c0_evac(5, 0)
+        c0_tr(5, 1)
+        stage1_act("x0", 7, 0)
+        stage1_act("x1", 3, 1)
+        c0_evac(5, 1)
+        c1_tr(0, 0, 0)
+        c0_tr(6, 0)
+        c0_quant(1, 1)
         stage1_act("x0", 7, 1)
+        c0_quant(2, 0)
+        c0_evac(6, 0)
+        c1_tr(0, 0, 1)
+        c1_evac(0, 0, 0)
+        c0_tr(6, 1)
+        c1_evac(0, 0, 1)
+        c0_evac(6, 1)
+        c1_tr(0, 0, 2)
+        c0_tr(7, 0)
+        c1_evac(0, 0, 2)
+        c0_evac(7, 0)
+        c0_tr(7, 1)
+        c1_tr(0, 0, 3)
+        c1_evac(0, 0, 3)
+        c0_evac(7, 1)
+        c1_tr(0, 1, 0)
+        c1_sum(0, 0, 0)
+        c0_quant(2, 1)
+        c1_evac(0, 1, 0)
+        c1_tr(0, 1, 1)
         stage1_mx("x1", 4, 0)
         stage1_mx("x1", 4, 1)
-        c1_tr(0, 0, 0)
-        c0_quant(0, 1)
-        stage1_act("x1", 4, 0)
-        c0_tr(5, 0)
         stage1_mx("x1", 5, 0)
-        c0_evac(4, 1)
-        c0_m(5)
-        stage1_act("x1", 4, 1)
         stage1_mx("x1", 5, 1)
-        c1_evac(0, 0, 0)
-        stage1_act("x1", 5, 0)
-        stage1_mx("x1", 6, 0)
-        c1_tr(0, 0, 1)
-        c0_tr(5, 1)
-        stage1_act("x1", 5, 1)
-        c0_evac(5, 0)
-        c0_quant(1, 0)
-        stage1_mx("x1", 6, 1)
-        stage1_act("x1", 6, 0)
-        c1_evac(0, 0, 1)
-        c0_m(6)
-        stage1_mx("x1", 7, 0)
-        c1_sum(0, 0, 0)
-        stage1_act("x1", 6, 1)
-        c0_tr(6, 0)
-        c1_tr(0, 0, 2)
-        stage1_mx("x1", 7, 1)
-        c0_evac(5, 1)
-        stage1_act("x1", 7, 0)
-        c0_quant(1, 1)
-        c1_evac(0, 0, 2)
-        stage1_act("x1", 7, 1)
-        c0_tr(6, 1)
-        c0_m(7)
-        c1_tr(0, 0, 3)
-        c0_evac(6, 0)
-        c1_m(4)
-        c1_sum(0, 0, 1)
-        c1_evac(0, 0, 3)
-        c0_quant(2, 0)
-        c0_tr(7, 0)
-        c0_evac(6, 1)
-        c1_tr(0, 1, 0)
-        c1_m(5)
-        c1_evac(0, 1, 0)
-        c0_tr(7, 1)
-        c1_m(6)
-        c0_evac(7, 0)
-        c0_quant(2, 1)
-        c1_tr(0, 1, 1)
-        norm_mm()
-        c1_sum(0, 0, 2)
         c1_evac(0, 1, 1)
-        c1_m(7)
-        c0_evac(7, 1)
+        stage1_mx("x1", 6, 0)
+        stage1_mx("x1", 6, 1)
+        c0_m(4)
+        stage1_mx("x1", 7, 0)
+        stage1_act("x1", 4, 0)
+        stage1_mx("x1", 7, 1)
+        stage1_act("x1", 4, 1)
+        stage1_act("x1", 5, 0)
+        stage1_act("x1", 5, 1)
+        c1_sum(0, 0, 1)
+        stage1_act("x1", 6, 0)
+        stage1_act("x1", 6, 1)
+        stage1_act("x1", 7, 0)
+        stage1_act("x1", 7, 1)
         c1_tr(0, 1, 2)
-        c0_quant(3, 0)
         c1_evac(0, 1, 2)
-        c1_sum(0, 0, 3)
+        c0_m(5)
         c1_tr(0, 1, 3)
-        c0_quant(3, 1)
+        c1_sum(0, 0, 2)
         c1_evac(0, 1, 3)
-        norm_take()
-        c1_sum(0, 1, 0)
-        c1_tr(1, 0, 0)
-        c1_tr(1, 0, 1)
-        c1_tr(1, 0, 2)
-        c1_tr(1, 0, 3)
+        c0_m(6)
+        c1_m(4)
+        c1_sum(0, 0, 3)
         c1_inter(0, 0)
-        c1_inter(0, 1)
-        c1_tr(1, 1, 0)
+        c1_m(5)
+        c0_m(7)
+        c0_quant(3, 0)
+        c1_m(6)
+        c1_tr(1, 0, 0)
+        c1_m(7)
+        c1_sum(0, 1, 0)
+        c1_tr(1, 0, 1)
         c1_sum(0, 1, 1)
-        c1_tr(1, 1, 1)
+        c1_tr(1, 0, 2)
+        c1_evac(1, 0, 0)
+        c1_inter(0, 1)
         c1_quant(0, 0)
+        c1_tr(1, 0, 3)
+        c1_sum(0, 1, 2)
+        c1_evac(1, 0, 1)
+        c1_tr(1, 1, 0)
+        c1_evac(1, 0, 2)
+        c1_sum(0, 1, 3)
+        c1_tr(1, 1, 1)
+        c1_evac(1, 0, 3)
         c1_tr(1, 1, 2)
         c1_quant(0, 1)
-        c1_evac(1, 0, 0)
         c1_tr(1, 1, 3)
-        c1_evac(1, 0, 1)
-        c1_evac(1, 0, 2)
-        c1_evac(1, 0, 3)
-        c1_sum(0, 1, 2)
-        c1_evac(1, 1, 0)
-        c1_evac(1, 1, 1)
-        c1_evac(1, 1, 2)
-        c1_evac(1, 1, 3)
         c1_inter(1, 0)
-        c1_sum(0, 1, 3)
+        c1_evac(1, 1, 0)
         stage2_mx(0, 0)
         m1_take(0)
-        c1_inter(1, 1)
+        c1_evac(1, 1, 1)
         stage2_mx(1, 0)
-        stage2_out(0, 0)
+        m1_spread(1)
+        c1_evac(1, 1, 2)
+        rank1(0, 0, "S")
         stage2_mx(2, 0)
+        c1_evac(1, 1, 3)
+        rank1(1, 0, "S")
+        c0_quant(3, 1)
+        m1_unspread(1)
+        c1_quant(1, 0)
+        rank1(2, 0, "S")
         stage2_mx(3, 0)
-        stage2_mx(4, 0)
+        rank1(3, 0, "S")
+        stage2_out(0, 0)
+        rank1(4, 0, "S")
+        c1_inter(1, 1)
+        rank1(5, 0, "P")
         stage2_out(1, 0)
-        stage2_mx(5, 0)
-        stage2_mx(6, 0)
-        stage2_mx(7, 0)
+        stage2_mx(4, 0)
+        rank1(6, 0, "P")
         stage2_out(2, 0)
+        rank1(7, 0, "P")
+        stage2_mx(5, 0)
         stage2_out(3, 0)
         stage2_out(4, 0)
-        c1_quant(1, 0)
-        c1_quant(1, 1)
+        stage2_mx(6, 0)
         stage2_out(5, 0)
-        scale_out(0, 0, "P")
-        planes_inter(0, 0, 0, 256, "S")
-        scale_out(1, 0, "P")
-        scale_out(2, 0, "P")
-        planes_inter(0, 0, 256, 512, "S")
+        c1_quant(1, 1)
         stage2_out(6, 0)
-        scale_out(3, 0, "P")
-        scale_out(4, 0, "P")
-        scale_out(5, 0, "P")
+        stage2_mx(7, 0)
         stage2_out(7, 0)
-        scale_out(6, 0, "P")
-        planes_quant(0, 0, 0, 512)
-        scale_out(7, 0, "P")
-        m1_spread(1)
+        rank1(0, 1, "P")
+        rank1(1, 1, "P")
+        rank1(2, 1, "P")
+        rank1(3, 1, "P")
+        rank1(4, 1, "P")
+        rank1(5, 1, "P")
+        rank1(6, 1, "P")
+        rank1(7, 1, "P")
         stage2_mx(0, 1)
+        planes_inter(0, 0, 0, 256, "S")
+        planes_inter(0, 0, 256, 512, "S")
         stage2_mx(1, 1)
-        stage2_mx(2, 1)
-        stage2_mx(3, 1)
-        m1_unspread(1)
-        stage2_mx(4, 1)
-        stage2_mx(5, 1)
-        planes_scales(0, 0)
         stage2_out(0, 1)
-        scale_out(0, 1, "P")
+        stage2_mx(2, 1)
         stage2_out(1, 1)
-        stage2_mx(6, 1)
-        scale_out(1, 1, "P")
+        stage2_mx(3, 1)
+        planes_quant(0, 0, 0, 512)
+        stage2_mx(4, 1)
         stage2_out(2, 1)
-        planes_inter(1, 0, 0, 256, "S")
-        stage2_mx(7, 1)
+        planes_scales(0, 0)
+        stage2_mx(5, 1)
         stage2_out(3, 1)
-        scale_out(2, 1, "P")
+        planes_inter(1, 0, 0, 256, "S")
+        stage2_mx(6, 1)
         stage2_out(4, 1)
         planes_inter(1, 0, 256, 512, "S")
-        planes_quant(1, 0, 0, 512)
+        stage2_mx(7, 1)
         stage2_out(5, 1)
-        planes_scales(1, 0)
-        scale_out(3, 1, "P")
+        planes_quant(1, 0, 0, 512)
         stage2_out(6, 1)
-        stage2_out(7, 1)
-        scale_out(4, 1, "P")
-        scale_out(5, 1, "P")
         planes_inter(0, 1, 0, 256, "S")
         planes_inter(0, 1, 256, 512, "S")
-        scale_out(6, 1, "V")
-        scale_out(7, 1, "P")
+        stage2_out(7, 1)
+        planes_scales(1, 0)
         planes_inter(1, 1, 0, 256, "V")
         planes_quant(0, 1, 0, 512)
         planes_scales(0, 1)
-        planes_quant(1, 1, 0, 256)
         planes_inter(1, 1, 256, 512, "S")
+        planes_quant(1, 1, 0, 256)
         planes_quant(1, 1, 256, 512)
         planes_scales(1, 1)

from contextlib import ExitStack

import concourse.mybir as mybir
from concourse.masks import make_identity

T, D, K = 1024, 512, 1024
P = 128
BUFS = {"ps": 7, "acc": 1}
FLOPS = 2 * (2 * T * D * K) + 2 * K * T * K

F32 = mybir.dt.float32
BF16 = mybir.dt.bfloat16
U32 = mybir.dt.uint32
I32 = mybir.dt.int32
U8 = mybir.dt.uint8
FP8X4 = mybir.dt.float8_e4m3fn_x4
FP4X4 = mybir.dt.float4_e2m1fn_x4
ADD = mybir.AluOpType.add
MUL = mybir.AluOpType.mult
TANH = mybir.ActivationFunctionType.Tanh
COPY = mybir.ActivationFunctionType.Copy
AX = mybir.AxisListType.X


def tile_girsanovreweightedneurallagcovariance_x2_kernel(
    tc, x0, x1, w_words, w_scales, bias, a, b, out_0, out_1, out_2
):
    nc = tc.nc
    with ExitStack() as ctx:
        keep = ctx.enter_context(tc.tile_pool(name="keep", bufs=1))
        work = ctx.enter_context(tc.tile_pool(name="work", bufs=2))
        psum = ctx.enter_context(tc.psum_pool(name="psum", bufs=1))
        ctx.enter_context(tc.manual_schedule())

        w_nat = keep.tile([P, 2 * K], U8, align_bytes=64)
        ws_nat = keep.tile([P, K], U8, align_bytes=64)
        nc.gpsimd.memset(ws_nat[:].bitcast(I32), 0)
        ident = keep.tile([P, P], F32)
        make_identity(nc, ident[:])
        ones = keep.tile([P, P], F32)
        nc.gpsimd.memset(ones[:], 1.0)
        neg_half = keep.tile([P, 1], F32)
        nc.gpsimd.memset(neg_half[:], -0.5)

        a_h = keep.tile([P, 8], BF16)
        b_h = keep.tile([P, 8], BF16)
        bias_h = keep.tile([P, 8], BF16)
        for t, v in ((a_h, a), (b_h, b)):
            nc.scalar.dma_start(out=t[:].rearrange("p (g j) -> p g j", g=2), in_=v.rearrange("(g p j) -> p g j", g=2, j=4))
        for q in range(4):
            nc.scalar.dma_start(
                out=ws_nat[32 * q : 32 * q + 4, :].bitcast(I32), in_=w_scales[0, 4 * q : 4 * q + 4, :].bitcast(I32)
            )
        nc.scalar.dma_start(out=bias_h[:].rearrange("p (g j) -> p g j", g=2), in_=bias.rearrange("(g p j) -> p g j", g=2, j=4))
        af = keep.tile([P, 8], F32)
        bf = keep.tile([P, 8], F32)
        pf = keep.tile([P, 8], F32)
        bias_f = keep.tile([P, 8], F32)
        xr = {}
        for name, x in (("x0", x0), ("x1", x1)):
            for g in range(2):
                t = keep.tile([P, 4, D], BF16, name="xr_%s_%d" % (name, g), align_bytes=64)
                xr[name, g] = t
                src = x[512 * g : 512 * g + 512, :].rearrange("(p j) d -> p j d", j=4)
                for jp in range(2):
                    nc.sync.dma_start(out=t[:, 2 * jp : 2 * jp + 2, :], in_=src[:, 2 * jp : 2 * jp + 2, :])
                    if (name, g, jp) == ("x0", 0, 0):
                        nc.sync.dma_start(out=w_nat[:].bitcast(I32), in_=w_words[0].bitcast(I32))

        nc.gpsimd.tensor_tensor(out=pf[:], in0=a_h[:], in1=b_h[:], op=MUL)
        for t, v in ((bias_f, bias_h), (af, a_h), (bf, b_h)):
            nc.gpsimd.tensor_copy(out=t[:], in_=v[:])

        w_perm = keep.tile([P, 2 * K], U8, align_bytes=64)
        ws_perm = keep.tile([P, K], U8, align_bytes=64)

        def permute(g, j0):
            nc.vector.tensor_copy(
                out=w_perm[:, 1024 * g + 256 * j0 : 1024 * g + 256 * j0 + 512].rearrange("p (j m b) -> p j m b", j=2, b=2),
                in_=w_nat[:, 1024 * g : 1024 * g + 1024].rearrange("p (m j b) -> p j m b", j=4, b=2)[:, j0 : j0 + 2],
            )
            nc.vector.tensor_copy(
                out=ws_perm[:, 512 * g + 128 * j0 : 512 * g + 128 * j0 + 256].rearrange("p (j m) -> p j m", j=2),
                in_=ws_nat[:, 512 * g : 512 * g + 512].rearrange("p (m j) -> p j m", j=4)[:, j0 : j0 + 2],
            )

        xq = {}
        xs = {}

        xbank = {}
        xt = {}

        def x_tr(name, g, jps):
            xw = xr[name, g][:].rearrange("p j d -> p (j d)").bitcast(F32)
            for jp in jps:
                bank = psum.tile([P, 512], F32, name="ps", bufs=BUFS["ps"])
                xbank[name, g, jp] = bank
                for jj in range(2):
                    for u in range(2):
                        j = 2 * jp + jj
                        nc.tensor.transpose(
                            bank[:, 256 * jj + 128 * u : 256 * jj + 128 * u + 128],
                            xw[:, 256 * j + u : 256 * (j + 1) : 2],
                            ident[:],
                        )

        def x_evac(name, g, jp, eng):
            if jp == 0:
                xt[name, g] = work.tile([P, 2048], BF16, name="xt", bufs=3, align_bytes=64)
            dst = xt[name, g][:].bitcast(F32)[:, 512 * jp : 512 * jp + 512].rearrange("p (j q u) -> p j q u", j=2, u=2)
            srcv = xbank[name, g, jp][:].rearrange("p (j u q) -> p j q u", j=2, u=2)
            if eng == "S":
                nc.scalar.copy(out=dst, in_=srcv)
            else:
                nc.vector.tensor_copy(out=dst, in_=srcv)

        def x_quant(name, g):
            cq = keep.tile([P, 512], U32, name="xq_%s_%d" % (name, g), align_bytes=64)
            cs = keep.tile([P, 512], U8, name="xs_%s_%d" % (name, g), align_bytes=64)
            nc.vector.quantize_mx(out=cq[:].bitcast(FP8X4), scales=cs[:], in_=xt[name, g][:])
            xq[name, g] = cq
            xs[name, g] = cs

        ct = {}
        ybank = {}

        def stage1_mx(name, k, g):
            bank = psum.tile([P, 512], F32, name="ps", bufs=BUFS["ps"])
            ybank[name, k, g] = bank
            nc.tensor.matmul_mx(
                out=bank[:],
                lhsT=w_perm[:, 256 * k : 256 * k + 256].bitcast(FP4X4),
                lhsT_scale=ws_perm[:, 128 * k : 128 * k + 128],
                rhs=xq[name, g][:].bitcast(FP8X4),
                rhs_scale=xs[name, g][:],
                start=True,
                stop=True,
            )

        def stage1_act(name, k, g):
            if g == 0:
                ct[name, k] = work.tile([P, 1024], F32, name="ct_" + name, bufs=8 if name == "x1" else 4)
            nc.scalar.activation(
                out=ct[name, k][:, 512 * g : 512 * g + 512],
                in_=ybank[name, k, g][:],
                func=TANH,
                bias=bias_f[:, k : k + 1],
                scale=1.0,
            )

        m0 = keep.tile([P, 8], F32)
        lq = [keep.tile([P, 1024], U32, name="lq_%d" % g, align_bytes=64) for g in range(2)]
        ls = [keep.tile([P, 1024], U8, name="ls_%d" % g, align_bytes=64) for g in range(2)]
        rq = [keep.tile([P, 1024], U32, name="rq_%d" % g, align_bytes=64) for g in range(2)]
        rsc = [keep.tile([P, 1024], U8, name="rsc_%d" % g, align_bytes=64) for g in range(2)]
        p_bc = keep.tile([P, 1024], F32)
        rs = keep.tile([P, 1], F32)
        nz = keep.tile([P, 1], F32)

        wbank = {}

        def weights_mm(h):
            bank = psum.tile([P, 512], F32, name="ps", bufs=BUFS["ps"])
            wbank[h] = bank
            for j in range(4):
                nc.tensor.matmul(
                    out=bank[:, 128 * j : 128 * j + 128],
                    lhsT=pf[:, 4 * h + j : 4 * h + j + 1].to_broadcast([P, P]),
                    rhs=ident[:],
                    start=True,
                    stop=True,
                )

        def weights_take(h):
            nc.scalar.copy(out=p_bc[:, 512 * h : 512 * h + 512], in_=wbank[h][:])

        nbank = {}

        def norm_mm():
            nbank[0] = psum.tile([P, 512], F32, name="ps", bufs=BUFS["ps"])
            nc.tensor.matmul(out=nbank[0][:, 0:8], lhsT=ones[:], rhs=pf[:], start=True, stop=True)

        def norm_take():
            p_sums = keep.tile([P, 8], F32)
            z = keep.tile([P, 1], F32)
            nc.scalar.activation(out=p_sums[:], in_=nbank[0][:, 0:8], func=COPY, accum_out=z[:])
            nc.gpsimd.tensor_tensor(out=rs[:], in0=z[:], in1=neg_half[:], op=mybir.AluOpType.pow)
            rs2 = keep.tile([P, 1], F32)
            nc.gpsimd.tensor_tensor(out=rs2[:], in0=rs[:], in1=rs[:], op=MUL)
            nc.gpsimd.tensor_scalar(out=nz[:], in0=rs2[:], scalar1=rs[:, 0:1], scalar2=-1.0, op0=MUL, op1=MUL)

        def c0_m(k):
            junk = work.tile([P, 1024], BF16, name="junk", bufs=2)
            nc.vector.scalar_tensor_tensor(
                out=junk[:], in0=ct["x0", k][:], scalar=1.0, in1=p_bc[:], op0=MUL, op1=MUL, accum_out=m0[:, k : k + 1]
            )

        lbf = {}
        banks = {}

        def c0_tr(k, g):
            bank = psum.tile([P, 512], F32, name="ps", bufs=BUFS["ps"])
            banks[k, g] = bank
            for j in range(4):
                col = 512 * g + 128 * j
                nc.tensor.transpose(bank[:, 128 * j : 128 * j + 128], ct["x0", k][:, col : col + 128], ident[:])

        def c0_evac(k, g):
            if k % 2 == 0:
                lbf[k // 2, g] = work.tile([P, 1024], BF16, name="lbf_%d" % g, bufs=2, align_bytes=64)
            o = 512 * (k % 2)
            nc.vector.tensor_tensor(
                out=lbf[k // 2, g][:, o : o + 512].rearrange("p (q j) -> p q j", j=4),
                in0=banks[k, g][:].rearrange("p (j q) -> p q j", j=4),
                in1=af[:, 4 * g : 4 * g + 4].unsqueeze(1).to_broadcast([P, P, 4]),
                op=MUL,
            )

        def c0_quant(kp, g):
            if True:
                nc.vector.quantize_mx(
                    out=lq[g][:, 256 * kp : 256 * kp + 256].bitcast(FP8X4),
                    scales=ls[g][:, 256 * kp : 256 * kp + 256],
                    in_=lbf[kp, g][:],
                )

        rf = {}

        c1_bank = {}

        def c1_tr(quad, g, j):
            bank = psum.tile([P, 512], F32, name="ps", bufs=BUFS["ps"])
            c1_bank[quad, g, j] = bank
            col = 512 * g + 128 * j
            for f in range(4):
                nc.tensor.transpose(
                    bank[:, 128 * f : 128 * f + 128], ct["x1", 4 * quad + f][:, col : col + 128], ident[:]
                )

        def c1_evac(quad, g, j):
            if j == 0:
                rf[quad, g] = work.tile([P, 4, 512], F32, name="rf", bufs=3)
            nc.scalar.activation(
                out=rf[quad, g][:, j, :].rearrange("p (q f) -> p q f", f=4),
                in_=c1_bank[quad, g, j][:].rearrange("p (f q) -> p q f", f=4),
                func=COPY,
                scale=bf[:, 4 * g + j : 4 * g + j + 1],
            )

        rbf = {}

        def c1_inter(quad, g):
            t = work.tile([P, 2048], BF16, name="rbf", bufs=2, align_bytes=64)
            rbf[quad, g] = t
            nc.vector.tensor_copy(
                out=t[:].rearrange("p (c i j) -> p c j i", i=4, j=4),
                in_=rf[quad, g][:].rearrange("p j (c i) -> p c j i", i=4),
            )

        acc = {}
        m1_bc = keep.tile([P, 1024], F32)

        def c1_sum(quad, g, j):
            if (g, j) == (0, 0):
                acc[quad] = psum.tile([P, 512], F32, name="acc", bufs=BUFS["acc"])
            nc.tensor.matmul(
                out=acc[quad][:],
                lhsT=af[:, 4 * g + j : 4 * g + j + 1].to_broadcast([P, P]),
                rhs=rf[quad, g][:, j, :],
                start=((g, j) == (0, 0)),
                stop=((g, j) == (1, 3)),
            )

        def m1_take(quad):
            nc.scalar.activation(
                out=m1_bc[:, 512 * quad : 512 * quad + 512], in_=acc[quad][:], func=COPY, scale=nz[:, 0:1]
            )

        m1 = keep.tile([P, 8], F32)

        def c1_m(k):
            junk = work.tile([P, 1024], BF16, name="junk", bufs=2)
            nc.vector.scalar_tensor_tensor(
                out=junk[:], in0=ct["x1", k][:], scalar=1.0, in1=p_bc[:], op0=MUL, op1=MUL, accum_out=m1[:, k : k + 1]
            )

        def c1_quant(quad, g):
            nc.vector.quantize_mx(
                out=rq[g][:, 512 * quad : 512 * quad + 512].bitcast(FP8X4),
                scales=rsc[g][:, 512 * quad : 512 * quad + 512],
                in_=rbf[quad, g][:],
            )

        spread = {}

        def m1_spread(quad):
            bank = psum.tile([P, 512], F32, name="ps", bufs=BUFS["ps"])
            for f in range(4):
                nc.tensor.matmul(
                    out=bank[:, 128 * f : 128 * f + 128],
                    lhsT=m1[:, 4 * quad + f : 4 * quad + f + 1].to_broadcast([P, P]),
                    rhs=ident[:],
                    start=True,
                    stop=True,
                )
            spread[quad] = bank

        def m1_unspread(quad):
            nc.scalar.activation(
                out=m1_bc[:, 512 * quad : 512 * quad + 512].rearrange("p (q f) -> p q f", f=4),
                in_=spread[quad][:].rearrange("p (f q) -> p q f", f=4),
                func=COPY,
                scale=nz[:, 0:1],
            )

        res = {}
        s_bank = {}

        def stage2_mx(k, h):
            mm = psum.tile([P, 512], F32, name="ps", bufs=BUFS["ps"])
            s_bank[k, h] = mm
            for g in range(2):
                nc.tensor.matmul_mx(
                    out=mm[:],
                    lhsT=lq[g][:, 128 * k : 128 * k + 128].bitcast(FP8X4),
                    lhsT_scale=ls[g][:, 128 * k : 128 * k + 128],
                    rhs=rq[g][:, 512 * h : 512 * h + 512].bitcast(FP8X4),
                    rhs_scale=rsc[g][:, 512 * h : 512 * h + 512],
                    start=(g == 0),
                    stop=(g == 1),
                )

        def stage2_out(k, h):
            quad, j = divmod(k, 4)
            if j == 0:
                res[quad, h] = work.tile([P, 4, 512], F32, name="res", bufs=4)
            nc.vector.scalar_tensor_tensor(
                out=res[quad, h][:, j, :], in0=s_bank[k, h][:], scalar=rs[:, 0:1], in1=gm[k, h][:], op0=MUL, op1=ADD
            )
            nc.sync.dma_start(
                out=out_0[512 * quad : 512 * quad + 512, :].rearrange("(p j) n -> p j n", j=4)[:, j, 512 * h : 512 * h + 512],
                in_=res[quad, h][:, j, :],
            )

        gm = {}

        def rank1(k, h, eng):
            gm[k, h] = work.tile([P, 512], F32, name="gm", bufs=8)
            row = m1_bc[:, 512 * h : 512 * h + 512]
            if eng == "S":
                nc.scalar.activation(out=gm[k, h][:], in_=row, func=COPY, scale=m0[:, k : k + 1])
            elif eng == "P":
                nc.gpsimd.tensor_scalar(
                    out=gm[k, h][:], in0=row, scalar1=m0[:, k : k + 1], scalar2=0.0, op0=MUL, op1=ADD
                )
            else:
                nc.vector.tensor_scalar(out=gm[k, h][:], in0=row, scalar1=m0[:, k : k + 1], scalar2=None, op0=MUL)

        ybf = {}
        yq = {}

        def planes_inter(quad, h, c0, c1, eng):
            if (quad, h) not in ybf:
                ybf[quad, h] = work.tile([P, 2048], BF16, name="ybf", bufs=2, align_bytes=64)
            dst = ybf[quad, h][:, 4 * c0 : 4 * c1].rearrange("p (c i j) -> p c j i", i=4, j=4)
            srcv = res[quad, h][:, :, c0:c1].rearrange("p j (c i) -> p c j i", i=4)
            if eng == "S":
                nc.scalar.copy(out=dst, in_=srcv)
            else:
                nc.vector.tensor_copy(out=dst, in_=srcv)

        def planes_quant(quad, h, c0, c1):
            if (quad, h) not in yq:
                yq[quad, h] = (
                    work.tile([P, 512], U32, name="yq", bufs=4, align_bytes=64),
                    work.tile([P, 512], U8, name="ys", bufs=4, align_bytes=64),
                )
            codes, scales = yq[quad, h]
            nc.vector.quantize_mx(
                out=codes[:, c0:c1].bitcast(FP8X4), scales=scales[:, c0:c1], in_=ybf[quad, h][:, 4 * c0 : 4 * c1]
            )
            nc.sync.dma_start(
                out=out_1[quad].rearrange("p m t -> p (m t)").bitcast(I32)[:, 512 * h + c0 : 512 * h + c1],
                in_=codes[:, c0:c1].bitcast(I32),
            )

        def planes_scales(quad, h):
            scales = yq[quad, h][1]
            for q in range(4):
                nc.sync.dma_start(
                    out=out_2[quad, 4 * q : 4 * q + 4, 512 * h : 512 * h + 512].bitcast(I32),
                    in_=scales[32 * q : 32 * q + 4, :].bitcast(I32),
                )

        warm_in = keep.tile([P, 512], BF16)
        nc.vector.memset(warm_in[:], 0.0)
        warm = psum.tile([P, 512], F32, name="acc", bufs=BUFS["acc"])
        for i in range(6):
            nc.tensor.matmul(out=warm[:], lhsT=warm_in[:, 0:P], rhs=warm_in[:], start=True, stop=True)
        x_tr("x0", 0, (0,))
        x_tr("x0", 0, (1,))
        x_tr("x0", 1, (0,))
        x_tr("x0", 1, (1,))
        x_evac("x0", 0, 0, "S")
        permute(0, 0)
        x_tr("x1", 0, (0,))
        x_tr("x1", 0, (1,))
        x_evac("x0", 1, 0, "S")
        x_evac("x0", 1, 1, "S")
        x_evac("x0", 0, 1, "V")
        x_evac("x1", 0, 0, "S")
        x_quant("x0", 0)
        stage1_mx("x0", 0, 0)
        weights_mm(0)
        weights_mm(1)
        permute(0, 2)
        x_tr("x1", 1, (0,))
        x_quant("x0", 1)
        x_evac("x1", 0, 1, "V")
        stage1_mx("x0", 0, 1)
        permute(1, 0)
        stage1_mx("x0", 1, 0)
        x_quant("x1", 0)
        stage1_act("x0", 0, 0)
        weights_take(0)
        norm_mm()
        x_tr("x1", 1, (1,))
        weights_take(1)
        stage1_mx("x0", 1, 1)
        x_evac("x1", 1, 0, "V")
        c0_tr(0, 0)
        stage1_act("x0", 0, 1)
        c0_tr(0, 1)
        permute(1, 2)
        stage1_mx("x0", 2, 0)
        stage1_act("x0", 1, 0)
        c0_m(0)
        x_evac("x1", 1, 1, "S")
        stage1_mx("x0", 2, 1)
        norm_take()
        stage1_mx("x0", 3, 0)
        stage1_act("x0", 1, 1)
        stage1_mx("x0", 3, 1)
        stage1_act("x0", 2, 0)
        c0_tr(1, 0)
        c0_evac(0, 0)
        stage1_act("x0", 2, 1)
        c0_evac(0, 1)
        stage1_act("x0", 3, 0)
        c0_tr(1, 1)
        stage1_act("x0", 3, 1)
        x_quant("x1", 1)
        c0_tr(2, 0)
        stage1_mx("x1", 0, 0)
        stage1_mx("x1", 0, 1)
        c0_tr(2, 1)
        stage1_act("x1", 0, 0)
        c0_evac(1, 0)
        c0_evac(1, 1)
        stage1_mx("x1", 1, 0)
        stage1_mx("x0", 4, 0)
        c0_tr(3, 0)
        c0_evac(2, 0)
        stage1_act("x1", 0, 1)
        c0_m(1)
        c0_evac(2, 1)
        stage1_mx("x0", 4, 1)
        stage1_mx("x1", 1, 1)
        c0_evac(3, 0)
        c0_quant(0, 0)
        c0_tr(3, 1)
        c0_quant(0, 1)
        stage1_act("x1", 1, 0)
        stage1_mx("x0", 5, 0)
        stage1_act("x0", 4, 0)
        c0_evac(3, 1)
        stage1_mx("x1", 2, 0)
        stage1_mx("x0", 5, 1)
        stage1_act("x0", 4, 1)
        c0_m(2)
        stage1_act("x1", 1, 1)
        stage1_mx("x1", 2, 1)
        stage1_mx("x0", 6, 0)
        c0_tr(4, 0)
        stage1_act("x0", 5, 0)
        stage1_act("x1", 2, 0)
        stage1_mx("x0", 6, 1)
        c0_evac(4, 0)
        stage1_act("x0", 5, 1)
        stage1_mx("x1", 3, 0)
        c0_tr(4, 1)
        c0_m(3)
        c0_quant(1, 0)
        stage1_mx("x0", 7, 0)
        stage1_act("x1", 2, 1)
        stage1_act("x0", 6, 0)
        c0_evac(4, 1)
        c0_tr(5, 0)
        stage1_mx("x1", 3, 1)
        stage1_mx("x0", 7, 1)
        stage1_act("x0", 6, 1)
        stage1_act("x1", 3, 0)
        c0_evac(5, 0)
        c0_tr(5, 1)
        stage1_act("x0", 7, 0)
        stage1_act("x1", 3, 1)
        c0_evac(5, 1)
        c1_tr(0, 0, 0)
        c0_tr(6, 0)
        c0_quant(1, 1)
        stage1_act("x0", 7, 1)
        c0_quant(2, 0)
        c0_evac(6, 0)
        c1_tr(0, 0, 1)
        c1_evac(0, 0, 0)
        c0_tr(6, 1)
        c1_evac(0, 0, 1)
        c0_evac(6, 1)
        c1_tr(0, 0, 2)
        c0_tr(7, 0)
        c1_evac(0, 0, 2)
        c0_evac(7, 0)
        c0_tr(7, 1)
        c1_tr(0, 0, 3)
        c1_evac(0, 0, 3)
        c0_evac(7, 1)
        c1_tr(0, 1, 0)
        c1_sum(0, 0, 0)
        c0_quant(2, 1)
        c1_evac(0, 1, 0)
        c1_tr(0, 1, 1)
        stage1_mx("x1", 4, 0)
        stage1_mx("x1", 4, 1)
        stage1_mx("x1", 5, 0)
        stage1_mx("x1", 5, 1)
        c1_evac(0, 1, 1)
        stage1_mx("x1", 6, 0)
        stage1_mx("x1", 6, 1)
        c0_m(4)
        stage1_mx("x1", 7, 0)
        stage1_act("x1", 4, 0)
        stage1_mx("x1", 7, 1)
        stage1_act("x1", 4, 1)
        stage1_act("x1", 5, 0)
        stage1_act("x1", 5, 1)
        c1_sum(0, 0, 1)
        stage1_act("x1", 6, 0)
        stage1_act("x1", 6, 1)
        stage1_act("x1", 7, 0)
        stage1_act("x1", 7, 1)
        c1_tr(0, 1, 2)
        c1_evac(0, 1, 2)
        c0_m(5)
        c1_tr(0, 1, 3)
        c1_sum(0, 0, 2)
        c1_evac(0, 1, 3)
        c0_m(6)
        c1_m(4)
        c1_sum(0, 0, 3)
        c1_inter(0, 0)
        c1_m(5)
        c0_m(7)
        c0_quant(3, 0)
        c1_m(6)
        c1_tr(1, 0, 0)
        c1_m(7)
        c1_sum(0, 1, 0)
        c1_tr(1, 0, 1)
        c1_sum(0, 1, 1)
        c1_tr(1, 0, 2)
        c1_evac(1, 0, 0)
        c1_inter(0, 1)
        c1_quant(0, 0)
        c1_tr(1, 0, 3)
        c1_sum(0, 1, 2)
        c1_evac(1, 0, 1)
        c1_tr(1, 1, 0)
        c1_evac(1, 0, 2)
        c1_sum(0, 1, 3)
        c1_tr(1, 1, 1)
        c1_evac(1, 0, 3)
        c1_tr(1, 1, 2)
        c1_quant(0, 1)
        c1_tr(1, 1, 3)
        c1_inter(1, 0)
        c1_evac(1, 1, 0)
        stage2_mx(0, 0)
        m1_take(0)
        c1_evac(1, 1, 1)
        stage2_mx(1, 0)
        m1_spread(1)
        c1_evac(1, 1, 2)
        rank1(0, 0, "S")
        stage2_mx(2, 0)
        c1_evac(1, 1, 3)
        rank1(1, 0, "S")
        c0_quant(3, 1)
        m1_unspread(1)
        c1_quant(1, 0)
        rank1(2, 0, "S")
        stage2_mx(3, 0)
        rank1(3, 0, "S")
        stage2_out(0, 0)
        rank1(4, 0, "S")
        c1_inter(1, 1)
        rank1(5, 0, "P")
        stage2_out(1, 0)
        stage2_mx(4, 0)
        rank1(6, 0, "P")
        stage2_out(2, 0)
        rank1(7, 0, "P")
        stage2_mx(5, 0)
        stage2_out(3, 0)
        stage2_out(4, 0)
        stage2_mx(6, 0)
        stage2_out(5, 0)
        c1_quant(1, 1)
        stage2_out(6, 0)
        stage2_mx(7, 0)
        stage2_out(7, 0)
        rank1(0, 1, "P")
        rank1(1, 1, "P")
        rank1(2, 1, "P")
        rank1(3, 1, "P")
        rank1(4, 1, "P")
        rank1(5, 1, "P")
        rank1(6, 1, "P")
        rank1(7, 1, "P")
        stage2_mx(0, 1)
        planes_inter(0, 0, 0, 256, "S")
        planes_inter(0, 0, 256, 512, "S")
        stage2_mx(1, 1)
        stage2_out(0, 1)
        stage2_mx(2, 1)
        stage2_out(1, 1)
        stage2_mx(3, 1)
        planes_quant(0, 0, 0, 512)
        stage2_mx(4, 1)
        stage2_out(2, 1)
        planes_scales(0, 0)
        stage2_mx(5, 1)
        stage2_out(3, 1)
        planes_inter(1, 0, 0, 256, "S")
        stage2_mx(6, 1)
        stage2_out(4, 1)
        planes_inter(1, 0, 256, 512, "S")
        stage2_mx(7, 1)
        stage2_out(5, 1)
        planes_quant(1, 0, 0, 512)
        stage2_out(6, 1)
        planes_inter(0, 1, 0, 256, "S")
        planes_inter(0, 1, 256, 512, "S")
        stage2_out(7, 1)
        planes_scales(1, 0)
        planes_inter(1, 1, 0, 256, "V")
        planes_quant(0, 1, 0, 512)
        planes_scales(0, 1)
        planes_inter(1, 1, 256, 512, "S")
        planes_quant(1, 1, 0, 256)
        planes_quant(1, 1, 256, 512)
        planes_scales(1, 1)
